import numpy as np
import ml_dtypes


def mxq(x, axis, fmt="e4m3"):
    dtype, down = {"e4m3": (ml_dtypes.float8_e4m3fn, 7), "e5m2": (ml_dtypes.float8_e5m2, 14)}[fmt]
    v = np.moveaxis(np.asarray(x, np.float32).astype(ml_dtypes.bfloat16).astype(np.float64), axis, -1)
    blocks = v.reshape(v.shape[:-1] + (-1, 32))
    amax = np.abs(blocks).max(-1, keepdims=True)
    byte = np.maximum(np.where(amax > 0, np.frexp(amax)[1] - 1 + 127, 0) - down, 1)
    scale = np.exp2(byte - 127.0)
    codes = (blocks / scale).astype(np.float32).astype(dtype).astype(np.float64)
    return np.moveaxis((codes * scale).reshape(v.shape), -1, axis)


WIDE = False


def mx_kscale(k):
    if not WIDE:
        return np.ones(k)
    levels = np.array([10, -10, 5, -5, 0])
    if k % 512:
        return np.exp2(np.random.permutation(np.resize(levels, k // 32))).repeat(32)
    a = np.empty((k // 512, 16))
    for p in range(k // 512):
        a[p, :8] = np.random.permutation(np.resize(levels, 8))
        for g in range(8):
            far = levels[np.abs(levels - a[p, g]) >= 10]
            a[p, g + 8] = far[np.random.randint(len(far))]
    return np.exp2(a.ravel()).repeat(32)


def f64(x):
    return np.asarray(x).astype(np.float64)


def striped(idx):
    return np.tile(idx.reshape(-1, 16).T, (8, 1)).astype(np.uint16)


def unstriped(offs):
    return offs[:16].T.reshape(-1).astype(np.int64)


E2M1 = np.array([0.0, 0.5, 1.0, 1.5, 2.0, 3.0, 4.0, 6.0, -0.0, -0.5, -1.0, -1.5, -2.0, -3.0, -4.0, -6.0])


def pack_weight(w, fmt):
    k, n = w.shape
    w = f64(np.asarray(w, np.float32).astype(ml_dtypes.bfloat16)).reshape(k // 32, 32, n)
    amax = np.abs(w).max(1)
    if fmt == "e4m3":
        byte = np.frexp(amax)[1] - 1 + 127 - 7
    else:
        mant, ex = np.frexp(amax / 6.0)
        byte = np.where(mant > 0.5, ex, ex - 1) + 127
    byte = np.clip(np.where(amax > 0, byte, 1), 1, 254)
    scaled = (w * np.exp2(127.0 - byte)[:, None, :]).reshape(k, n).astype(np.float32)
    by_word = np.ascontiguousarray(scaled.reshape(k // 512, 128, 4, n).transpose(0, 1, 3, 2))
    if fmt == "e4m3":
        words = by_word.astype(ml_dtypes.float8_e4m3fn).view(np.uint8)
    else:
        c = by_word.astype(ml_dtypes.float4_e2m1fn).view(np.uint8) & 0xF
        words = (c[..., 0::2] | (c[..., 1::2] << 4)).reshape(k // 512, 128, 2 * n)
    return np.ascontiguousarray(words), np.ascontiguousarray(byte.astype(np.uint8).reshape(k // 512, 16, n))


def unpack_weight(words, scales, fmt):
    g, _, n = scales.shape
    words = np.ascontiguousarray(words).reshape(g, 128, n, -1)
    if fmt == "e4m3":
        vals = words.view(ml_dtypes.float8_e4m3fn).astype(np.float64)
    else:
        nib = np.empty((g, 128, n, 4), np.uint8)
        nib[..., 0::2] = words & 0xF
        nib[..., 1::2] = words >> 4
        vals = E2M1[nib]
    vals = vals * np.repeat(np.exp2(scales.astype(np.float64) - 127.0), 8, axis=1)[..., None]
    return vals.transpose(0, 1, 3, 2).reshape(g * 512, n)


def silu(v):
    return v / (1.0 + np.exp(-np.maximum(v, -700.0)))


K, T, E, C, H, N = 1536, 512, 2, 256, 512, 256


def by_expert(wq, xq):
    return np.concatenate([wq[e].T @ xq[:, e * C:(e + 1) * C] for e in range(E)], axis=1)


def setup_inputs():
    n = np.random.standard_normal
    s = mx_kscale(K)[:, None]
    u = mx_kscale(H)
    w1 = [pack_weight(m, "e2m1") for m in n((E, K, H)) / np.sqrt(K) / s[None] * u[None, None, :]]
    w2 = [pack_weight(m, "e2m1") for m in n((E, H, N)) / np.sqrt(H) / u[None, :, None]]
    return {
        "xT": (n((K, T)) * s).astype(np.float32),
        "w1_words": np.stack([m[0] for m in w1]),
        "w1_scales": np.stack([m[1] for m in w1]),
        "w2_words": np.stack([m[0] for m in w2]),
        "w2_scales": np.stack([m[1] for m in w2]),
        "gate": np.tile(np.random.uniform(0.2, 1.0, E * C), (N, 1)).astype(np.float32),
        "offs": striped(np.random.permutation(T)[:E * C]),
        "dst": striped(np.random.permutation(T)[:E * C]),
    }


def reference(xT, w1_words, w1_scales, w2_words, w2_scales, gate, offs, dst):
    idx = unstriped(offs)
    w1 = np.stack([unpack_weight(w1_words[e], w1_scales[e], "e2m1") for e in range(E)])
    w2 = np.stack([unpack_weight(w2_words[e], w2_scales[e], "e2m1") for e in range(E)])
    xq = mxq(f64(xT)[:, idx], 0, "e4m3")
    h = silu(by_expert(w1, xq))
    y = by_expert(w2, mxq(h, 0, "e4m3"))
    out = np.zeros((N, T))
    out[:, unstriped(dst)] = f64(gate) * y
    return out

@@ -1,0 +1,252 @@
+from contextlib import ExitStack
+
+import concourse.mybir as mybir
+from concourse.masks import make_identity
+
+K, T, E, C, H, N = 1536, 512, 2, 256, 512, 256
+FLOPS = 2 * E * C * (K * H + H * N)
+
+F32 = mybir.dt.float32
+BF16 = mybir.dt.bfloat16
+I32 = mybir.dt.int32
+U32 = mybir.dt.uint32
+U16 = mybir.dt.uint16
+U8 = mybir.dt.uint8
+E4M3 = mybir.dt.float8_e4m3fn_x4
+E2M1 = mybir.dt.float4_e2m1fn_x4
+
+P = 128
+PASSES = K // 512
+HALF = T // 2
+COPY = mybir.ActivationFunctionType.Copy
+SILU = mybir.ActivationFunctionType.Silu
+MULT = mybir.AluOpType.mult
+
+
+def interleave_views(dst, src):
+    return (
+        dst.rearrange("p (c i) j -> p c j i", i=4),
+        src.rearrange("p j (c i) -> p c j i", i=4),
+    )
+
+
+def tile_moe_two_mlp_silu_kernel(
+    tc, xT, w1_words, w1_scales, w2_words, w2_scales, gate, offs, dst, out
+):
+    nc = tc.nc
+    with ExitStack() as ctx:
+        keep = ctx.enter_context(tc.tile_pool(name="keep", bufs=1))
+        psum = ctx.enter_context(tc.psum_pool(name="psum", bufs=1))
+
+        offs_t = keep.tile([P, T // 16], U16, name="offs_t")
+        dst_t = keep.tile([P, T // 16], U16, name="dst_t")
+        w1_sc = keep.tile([P, E * PASSES, H], U8, name="w1_sc", align_bytes=64)
+        w2_sc = keep.tile([P, E, N], U8, name="w2_sc", align_bytes=64)
+        nc.vector.memset(w1_sc[:].rearrange("p e i -> p (e i)").bitcast(I32), 0)
+        nc.vector.memset(w2_sc[:].rearrange("p e i -> p (e i)").bitcast(I32), 0)
+
+        scales = [keep.tile([P, T], U8, name=f"scales{s}", align_bytes=64) for s in range(PASSES)]
+        for s in range(PASSES):
+            nc.gpsimd.memset(scales[s][:].bitcast(I32), 0)
+
+        raw = {}
+
+        def load_x(s, half):
+            rows = xT[512 * s : 512 * (s + 1), :].rearrange("(p j) t -> p j t", j=4)
+            tile = keep.tile([P, 4, HALF], F32, name=f"raw{s}_{half}")
+            nc.sync.dma_start(tile[:], rows[:, :, HALF * half : HALF * (half + 1)])
+            raw[s, half] = tile
+
+        w1_t = {}
+
+        def load_w1(s):
+            tile = keep.tile([P, E, 2 * H], U8, name=f"w1_{s}", align_bytes=64)
+            nc.sync.dma_start(tile[:], w1_words[:, s].rearrange("e p c -> p e c"))
+            for e in range(E):
+                w1_t[e, s] = tile[:, e, :]
+
+        load_x(0, 0)
+        load_x(0, 1)
+        nc.sync.dma_start(offs_t[:], offs)
+        load_x(1, 0)
+        load_x(1, 1)
+        for q in range(4):
+            nc.sync.dma_start(
+                w1_sc[32 * q : 32 * q + 4].bitcast(I32),
+                w1_scales[:, :, 4 * q : 4 * q + 4, :].rearrange("e s q i -> q (e s) i").bitcast(I32),
+            )
+        load_w1(0)
+        load_x(2, 0)
+        load_x(2, 1)
+        load_w1(1)
+        load_w1(2)
+        w2_t = keep.tile([P, E, 2 * N], U8, name="w2_t", align_bytes=64)
+        gate_t = keep.tile([P, 2, T], F32, name="gate_t")
+
+        for q in range(4):
+            nc.sync.dma_start(
+                w2_sc[32 * q : 32 * q + 4].bitcast(I32),
+                w2_scales[:, 0, 4 * q : 4 * q + 4, :].rearrange("e q n -> q e n").bitcast(I32),
+            )
+        nc.sync.dma_start(w2_t[:], w2_words.rearrange("e s p c -> p (e s) c"))
+        nc.sync.dma_start(dst_t[:], dst)
+        nc.sync.dma_start(gate_t[:], gate.rearrange("(h p) j -> p h j", h=2))
+
+        ident = keep.tile([P, P], F32, name="ident")
+        make_identity(nc, ident[:])
+        warm = keep.tile([P, 1], F32, name="warm")
+        nc.gpsimd.memset(warm[:], 0.0)
+        warm_out = keep.tile([P, 1], F32, name="warm_out")
+        nc.scalar.activation(warm_out[:], warm[:], SILU)
+
+
+        acc = [psum.tile([P, H], F32, name=f"acc{b}") for b in range(4)]
+        turned = [psum.tile([P, 2, P], F32, name=f"turned{b}") for b in range(2)]
+        y = [psum.tile([P, 2, C], F32, name=f"y{i}") for i in range(2)]
+
+        words = [keep.tile([P, T], U32, name=f"words{s}", align_bytes=64) for s in range(PASSES)]
+        gw = {}
+        gs = {}
+
+        def quantise(s, half, vector_from):
+            parts = [(nc.scalar, 0, vector_from), (nc.vector, vector_from, HALF)]
+            for engine, t0, t1 in parts:
+                if t0 == t1:
+                    continue
+                grouped = keep.tile([P, t1 - t0, 4], BF16, name=f"grouped{s}_{half}_{t0}", tag=f"grouped{s}_{half}_{t0}", align_bytes=64)
+                to, frm = interleave_views(grouped[:], raw[s, half][:, :, t0:t1])
+                if engine is nc.scalar:
+                    nc.scalar.activation(to, frm, COPY)
+                else:
+                    nc.vector.tensor_copy(to, frm)
+                cols = slice(HALF * half + t0, HALF * half + t1)
+                nc.vector.quantize_mx(
+                    out=words[s][:, cols].bitcast(E4M3),
+                    scales=scales[s][:, cols],
+                    in_=grouped[:].rearrange("p t j -> p (t j)"),
+                )
+
+        def gather_words(s, c0, c1):
+            w = keep.tile([P, c1 - c0], U32, name=f"gw{s}_{c0}", align_bytes=64)
+            nc.vector.tensor_copy(w[:], words[s][:].indirect(offs_t[:, c0 // 16 : c1 // 16]))
+            for b in range(c0 // P, c1 // P):
+                gw[s, b] = w[:, P * b - c0 : P * b - c0 + P]
+
+        def gather_scales(s, c0, c1, tag=None):
+            name = f"gs{s}_{c0}"
+            g = keep.tile([P, c1 - c0], U8, name=name, tag=name if tag is None else tag, align_bytes=64)
+            nc.vector.tensor_copy(g[:], scales[s][:].indirect(offs_t[:, c0 // 16 : c1 // 16]))
+            for b in range(c0 // P, c1 // P):
+                gs[s, b] = g[:, P * b - c0 : P * b - c0 + P]
+
+        def first_layer(s, b):
+            e = b // 2
+            nc.tensor.matmul_mx(
+                out=acc[b][:],
+                lhsT=gw[s, b].bitcast(E4M3),
+                lhsT_scale=gs[s, b],
+                rhs=w1_t[e, s].bitcast(E2M1),
+                rhs_scale=w1_sc[:, e * PASSES + s, :],
+                start=(s == 0),
+                stop=(s == PASSES - 1),
+            )
+
+        h_t = {}
+
+        def activate(b):
+            h = keep.tile([P, H], BF16, name=f"h{b}")
+            nc.scalar.activation(h[:], acc[b][:], SILU)
+            h_t[b] = h
+
+        def turn(b):
+            h_pairs = h_t[b][:].bitcast(F32)
+            for u in range(2):
+                nc.tensor.transpose(turned[b % 2][:, u, :], h_pairs[:, u::2], ident[:])
+
+        grouped_h = {}
+
+        def regroup(b, c0, c1):
+            if c0 not in grouped_h:
+                grouped_h[c0] = keep.tile([P, c1 - c0, 4], BF16, name=f"hgrouped{c0}", align_bytes=64)
+            pairs = grouped_h[c0][:].rearrange("p r f -> p (r f)").bitcast(F32).rearrange("p (r u) -> p r u", u=2)
+            nc.scalar.copy(pairs[:, P * b - c0 : P * b - c0 + P, :], turned[b % 2][:].rearrange("p u r -> p r u"))
+
+        windows = [keep.tile([P, T], F32, name=f"window{nh}") for nh in range(2)]
+        ysb = {}
+
+        def second_layer(c0, c1, bank):
+            e, n = c0 // C, c1 - c0
+            hw = keep.tile([P, n], U32, name=f"hw{c0}", align_bytes=64)
+            hsc = keep.tile([P, n], U8, name=f"hsc{c0}", align_bytes=64)
+            nc.vector.quantize_mx(
+                out=hw[:].bitcast(E4M3), scales=hsc[:], in_=grouped_h[c0][:].rearrange("p r f -> p (r f)")
+            )
+            for nh in range(2):
+                nc.tensor.matmul_mx(
+                    out=y[bank][:, nh, 0:n],
+                    lhsT=w2_t[:, e, N * nh : N * (nh + 1)].bitcast(E2M1),
+                    lhsT_scale=w2_sc[:, e, P * nh : P * (nh + 1)],
+                    rhs=hw[:].bitcast(E4M3),
+                    rhs_scale=hsc[:],
+                    start=True,
+                    stop=True,
+                )
+            for nh in range(2):
+                yt = keep.tile([P, n], F32, name=f"ysb{c0}_{nh}")
+                nc.scalar.activation(yt[:], y[bank][:, nh, 0:n], COPY)
+                ysb[c0, nh] = yt
+
+        def scatter(c0, c1):
+            for nh in range(2):
+                nc.vector.tensor_tensor(
+                    windows[nh][:].indirect(dst_t[:, c0 // 16 : c1 // 16]),
+                    ysb[c0, nh][:],
+                    gate_t[:, nh, c0:c1],
+                    MULT,
+                )
+
+        quantise(0, 0, P)
+        quantise(0, 1, P)
+        gather_words(0, 0, C)
+        gather_scales(0, 0, C)
+        for b in range(2):
+            first_layer(0, b)
+        gather_words(0, C, T)
+        quantise(1, 0, HALF)
+        quantise(1, 1, HALF)
+        gather_scales(0, C, T, tag="grouped1_0_0")
+        for b in range(2, 4):
+            first_layer(0, b)
+        gather_words(1, 0, C)
+        gather_scales(1, 0, C)
+        for b in range(2):
+            first_layer(1, b)
+        gather_words(1, C, T)
+        quantise(2, 0, HALF)
+        quantise(2, 1, HALF)
+        gather_scales(1, C, T, tag="grouped2_0_0")
+        for b in range(2, 4):
+            first_layer(1, b)
+        for b in range(2):
+            gather_words(2, P * b, P * (b + 1))
+            gather_scales(2, P * b, P * (b + 1))
+            first_layer(2, b)
+            activate(b)
+            turn(b)
+            regroup(b, P * b, P * (b + 1))
+        gather_words(2, C, T)
+        gather_scales(2, C, T)
+        second_layer(0, P, 0)
+        second_layer(P, C, 1)
+        first_layer(2, 2)
+        first_layer(2, 3)
+        scatter(0, P)
+        for b in range(2, 4):
+            activate(b)
+            turn(b)
+            regroup(b, C, T)
+        second_layer(C, T, 0)
+        scatter(P, C)
+        scatter(C, T)
+        for nh in range(2):
+            nc.sync.dma_start(out[P * nh : P * (nh + 1), :], windows[nh][:])

@@ -18,6 +18,7 @@ E2M1 = mybir.dt.float4_e2m1fn_x4
 P = 128
 PASSES = K // 512
 HALF = T // 2
+ORDERS = ((1, 0, 2), (0, 1, 2), (2, 1, 0), (2, 1, 0))
 COPY = mybir.ActivationFunctionType.Copy
 SILU = mybir.ActivationFunctionType.Silu
 MULT = mybir.AluOpType.mult
@@ -45,52 +46,55 @@ def tile_moe_two_mlp_silu_kernel(
         nc.vector.memset(w1_sc[:].rearrange("p e i -> p (e i)").bitcast(I32), 0)
         nc.vector.memset(w2_sc[:].rearrange("p e i -> p (e i)").bitcast(I32), 0)
 
-        scales = [keep.tile([P, T], U8, name=f"scales{s}", align_bytes=64) for s in range(PASSES)]
-        for s in range(PASSES):
-            nc.gpsimd.memset(scales[s][:].bitcast(I32), 0)
+        scales01 = keep.tile([P, T], U8, name="scales01", align_bytes=64)
+        scales2 = keep.tile([P, T], U8, name="scales2", align_bytes=64)
+        moved0 = keep.tile([P, T], U8, name="moved0", align_bytes=64)
+        for plane in (scales01, scales2, moved0):
+            nc.gpsimd.memset(plane[:].bitcast(I32), 0)
+        scales = [scales01[4:P], scales01[:], scales2[:]]
 
         raw = {}
 
         def load_x(s, half):
             rows = xT[512 * s : 512 * (s + 1), :].rearrange("(p j) t -> p j t", j=4)
-            tile = keep.tile([P, 4, HALF], F32, name=f"raw{s}_{half}")
+            tile = keep.tile([P, 4, HALF], F32, name=f"raw{s}_{half}", tag=f"raw{s}_{half}", align_bytes=64)
             nc.sync.dma_start(tile[:], rows[:, :, HALF * half : HALF * (half + 1)])
             raw[s, half] = tile
 
         w1_t = {}
 
-        def load_w1(s):
-            tile = keep.tile([P, E, 2 * H], U8, name=f"w1_{s}", align_bytes=64)
-            nc.sync.dma_start(tile[:], w1_words[:, s].rearrange("e p c -> p e c"))
-            for e in range(E):
-                w1_t[e, s] = tile[:, e, :]
+        def load_w1(e, s0, s1):
+            tile = keep.tile([P, s1 - s0, 2 * H], U8, name=f"w1_{e}_{s0}", align_bytes=64)
+            nc.sync.dma_start(tile[:], w1_words[e, s0:s1].rearrange("s p c -> p s c"))
+            for s in range(s0, s1):
+                w1_t[e, s] = tile[:, s - s0, :]
 
         load_x(0, 0)
         load_x(0, 1)
         nc.sync.dma_start(offs_t[:], offs)
         load_x(1, 0)
         load_x(1, 1)
+        load_x(2, 0)
+        load_x(2, 1)
         for q in range(4):
             nc.sync.dma_start(
                 w1_sc[32 * q : 32 * q + 4].bitcast(I32),
                 w1_scales[:, :, 4 * q : 4 * q + 4, :].rearrange("e s q i -> q (e s) i").bitcast(I32),
             )
-        load_w1(0)
-        load_x(2, 0)
-        load_x(2, 1)
-        load_w1(1)
-        load_w1(2)
+        load_w1(0, 0, PASSES)
         w2_t = keep.tile([P, E, 2 * N], U8, name="w2_t", align_bytes=64)
-        gate_t = keep.tile([P, 2, T], F32, name="gate_t")
+        gate_t = keep.tile([P, T], F32, name="gate_t")
 
-        for q in range(4):
-            nc.sync.dma_start(
-                w2_sc[32 * q : 32 * q + 4].bitcast(I32),
-                w2_scales[:, 0, 4 * q : 4 * q + 4, :].rearrange("e q n -> q e n").bitcast(I32),
-            )
-        nc.sync.dma_start(w2_t[:], w2_words.rearrange("e s p c -> p (e s) c"))
-        nc.sync.dma_start(dst_t[:], dst)
-        nc.sync.dma_start(gate_t[:], gate.rearrange("(h p) j -> p h j", h=2))
+        def late_loads():
+            nc.sync.dma_start(dst_t[:], dst)
+            for q in range(4):
+                nc.sync.dma_start(
+                    w2_sc[32 * q : 32 * q + 4].bitcast(I32),
+                    w2_scales[:, 0, 4 * q : 4 * q + 4, :].rearrange("e q n -> q e n").bitcast(I32),
+                )
+            load_w1(1, 0, PASSES)
+            nc.sync.dma_start(w2_t[:], w2_words.rearrange("e s p c -> p (e s) c"))
+            nc.sync.dma_start(gate_t[:], gate[0:P, :])
 
         ident = keep.tile([P, P], F32, name="ident")
         make_identity(nc, ident[:])
@@ -99,91 +103,100 @@ def tile_moe_two_mlp_silu_kernel(
         warm_out = keep.tile([P, 1], F32, name="warm_out")
         nc.scalar.activation(warm_out[:], warm[:], SILU)
 
-
-        acc = [psum.tile([P, H], F32, name=f"acc{b}") for b in range(4)]
-        turned = [psum.tile([P, 2, P], F32, name=f"turned{b}") for b in range(2)]
-        y = [psum.tile([P, 2, C], F32, name=f"y{i}") for i in range(2)]
-
         words = [keep.tile([P, T], U32, name=f"words{s}", align_bytes=64) for s in range(PASSES)]
         gw = {}
         gs = {}
 
         def quantise(s, half, vector_from):
-            parts = [(nc.scalar, 0, vector_from), (nc.vector, vector_from, HALF)]
-            for engine, t0, t1 in parts:
+            grouped = keep.tile([P, HALF, 4], BF16, name=f"grouped{s}_{half}", tag=f"grouped{s}_{half}", align_bytes=64)
+            for engine, t0, t1 in [(nc.scalar, 0, vector_from), (nc.vector, vector_from, HALF)]:
                 if t0 == t1:
                     continue
-                grouped = keep.tile([P, t1 - t0, 4], BF16, name=f"grouped{s}_{half}_{t0}", tag=f"grouped{s}_{half}_{t0}", align_bytes=64)
-                to, frm = interleave_views(grouped[:], raw[s, half][:, :, t0:t1])
+                to, frm = interleave_views(grouped[:, t0:t1, :], raw[s, half][:, :, t0:t1])
                 if engine is nc.scalar:
                     nc.scalar.activation(to, frm, COPY)
                 else:
                     nc.vector.tensor_copy(to, frm)
-                cols = slice(HALF * half + t0, HALF * half + t1)
-                nc.vector.quantize_mx(
-                    out=words[s][:, cols].bitcast(E4M3),
-                    scales=scales[s][:, cols],
-                    in_=grouped[:].rearrange("p t j -> p (t j)"),
-                )
+            cols = slice(HALF * half, HALF * (half + 1))
+            nc.vector.quantize_mx(
+                out=words[s][:, cols].bitcast(E4M3),
+                scales=scales[s][:, cols],
+                in_=grouped[:].rearrange("p t j -> p (t j)"),
+            )
 
-        def gather_words(s, c0, c1):
-            w = keep.tile([P, c1 - c0], U32, name=f"gw{s}_{c0}", align_bytes=64)
+        def gather_words(s, c0, c1, tag=None):
+            name = f"gw{s}_{c0}"
+            w = keep.tile([P, c1 - c0], U32, name=name, tag=name if tag is None else tag, align_bytes=64)
             nc.vector.tensor_copy(w[:], words[s][:].indirect(offs_t[:, c0 // 16 : c1 // 16]))
             for b in range(c0 // P, c1 // P):
                 gw[s, b] = w[:, P * b - c0 : P * b - c0 + P]
 
-        def gather_scales(s, c0, c1, tag=None):
-            name = f"gs{s}_{c0}"
-            g = keep.tile([P, c1 - c0], U8, name=name, tag=name if tag is None else tag, align_bytes=64)
-            nc.vector.tensor_copy(g[:], scales[s][:].indirect(offs_t[:, c0 // 16 : c1 // 16]))
+        def gather_scales2(c0, c1):
+            g = keep.tile([P, c1 - c0], U8, name=f"gs2_{c0}", align_bytes=64)
+            nc.vector.tensor_copy(g[:], scales2[:].indirect(offs_t[:, c0 // 16 : c1 // 16]))
             for b in range(c0 // P, c1 // P):
-                gs[s, b] = g[:, P * b - c0 : P * b - c0 + P]
+                gs[2, b] = g[:, P * b - c0 : P * b - c0 + P]
+
+        def gather_scales01(c0, tag):
+            g = keep.tile([P, C], U8, name=f"gs01_{c0}", tag=tag, align_bytes=64)
+            nc.vector.tensor_copy(g[:], scales01[:].indirect(offs_t[:, c0 // 16 : (c0 + C) // 16]))
+            nc.sync.dma_start(moved0[0:100, c0 : c0 + C].bitcast(I32), g[4:104].bitcast(I32))
+            for b in range(c0 // P, (c0 + C) // P):
+                gs[1, b] = g[:, P * b - c0 : P * b - c0 + P]
+                gs[0, b] = moved0[:, P * b : P * (b + 1)]
+
+        acc = {}
 
         def first_layer(s, b):
             e = b // 2
+            if s == ORDERS[b][0]:
+                acc[b] = psum.tile([P, H], F32, name=f"acc{b}", tag=f"bank{b}")
             nc.tensor.matmul_mx(
                 out=acc[b][:],
                 lhsT=gw[s, b].bitcast(E4M3),
                 lhsT_scale=gs[s, b],
                 rhs=w1_t[e, s].bitcast(E2M1),
                 rhs_scale=w1_sc[:, e * PASSES + s, :],
-                start=(s == 0),
-                stop=(s == PASSES - 1),
+                start=(s == ORDERS[b][0]),
+                stop=(s == ORDERS[b][-1]),
             )
-
-        h_t = {}
-
-        def activate(b):
-            h = keep.tile([P, H], BF16, name=f"h{b}")
-            nc.scalar.activation(h[:], acc[b][:], SILU)
-            h_t[b] = h
-
-        def turn(b):
-            h_pairs = h_t[b][:].bitcast(F32)
-            for u in range(2):
-                nc.tensor.transpose(turned[b % 2][:, u, :], h_pairs[:, u::2], ident[:])
 
         grouped_h = {}
+        h_t = {}
+        hw_t = {}
 
-        def regroup(b, c0, c1):
-            if c0 not in grouped_h:
-                grouped_h[c0] = keep.tile([P, c1 - c0, 4], BF16, name=f"hgrouped{c0}", align_bytes=64)
-            pairs = grouped_h[c0][:].rearrange("p r f -> p (r f)").bitcast(F32).rearrange("p (r u) -> p r u", u=2)
-            nc.scalar.copy(pairs[:, P * b - c0 : P * b - c0 + P, :], turned[b % 2][:].rearrange("p u r -> p r u"))
+        def hidden(b):
+            h = keep.tile([P, H], BF16, name=f"h{b}", tag=f"h{b}")
+            nc.scalar.activation(
+                h[:].rearrange("r (u p d) -> r u p d", u=2, d=2),
+                acc[b][:].rearrange("r (p u d) -> r u p d", u=2, d=2),
+                SILU,
+            )
+            h_pairs = h[:].bitcast(F32)
+            h_t[b] = h
+            turned = psum.tile([P, 2, P], F32, name=f"turned{b}", tag=f"bank{(b + 2) % 4}")
+            for u in range(2):
+                nc.tensor.transpose(turned[:, u, :], h_pairs[:, P * u : P * (u + 1)], ident[:])
+            grouped_h[b] = keep.tile([P, P, 4], BF16, name=f"hgrouped{b}", tag=f"hgrouped{b}", align_bytes=64)
+            pairs = grouped_h[b][:].rearrange("p r f -> p (r f)").bitcast(F32).rearrange("p (r u) -> p r u", u=2)
+            nc.scalar.copy(pairs, turned[:].rearrange("p u r -> p r u"))
 
         windows = [keep.tile([P, T], F32, name=f"window{nh}") for nh in range(2)]
+        y = {}
         ysb = {}
 
-        def second_layer(c0, c1, bank):
-            e, n = c0 // C, c1 - c0
-            hw = keep.tile([P, n], U32, name=f"hw{c0}", align_bytes=64)
-            hsc = keep.tile([P, n], U8, name=f"hsc{c0}", align_bytes=64)
+        def second_layer(b):
+            e = b // 2
+            hw = keep.tile([P, P], U32, name=f"hw{b}", align_bytes=64)
+            hsc = keep.tile([P, P], U8, name=f"hsc{b}", tag=f"hsc{b}", align_bytes=64)
             nc.vector.quantize_mx(
-                out=hw[:].bitcast(E4M3), scales=hsc[:], in_=grouped_h[c0][:].rearrange("p r f -> p (r f)")
+                out=hw[:].bitcast(E4M3), scales=hsc[:], in_=grouped_h[b][:].rearrange("p r f -> p (r f)")
             )
+            hw_t[b] = hw
+            y[b] = psum.tile([P, 2, P], F32, name=f"y{b}")
             for nh in range(2):
                 nc.tensor.matmul_mx(
-                    out=y[bank][:, nh, 0:n],
+                    out=y[b][:, nh, :],
                     lhsT=w2_t[:, e, N * nh : N * (nh + 1)].bitcast(E2M1),
                     lhsT_scale=w2_sc[:, e, P * nh : P * (nh + 1)],
                     rhs=hw[:].bitcast(E4M3),
@@ -191,62 +204,66 @@ def tile_moe_two_mlp_silu_kernel(
                     start=True,
                     stop=True,
                 )
-            for nh in range(2):
-                yt = keep.tile([P, n], F32, name=f"ysb{c0}_{nh}")
-                nc.scalar.activation(yt[:], y[bank][:, nh, 0:n], COPY)
-                ysb[c0, nh] = yt
 
-        def scatter(c0, c1):
-            for nh in range(2):
-                nc.vector.tensor_tensor(
-                    windows[nh][:].indirect(dst_t[:, c0 // 16 : c1 // 16]),
-                    ysb[c0, nh][:],
-                    gate_t[:, nh, c0:c1],
-                    MULT,
-                )
+        def leave(b, nh, tag=None):
+            name = f"ysb{b}_{nh}"
+            yt = keep.tile([P, P], F32, name=name, tag=name if tag is None else tag)
+            nc.scalar.activation(yt[:], y[b][:, nh, :], COPY)
+            ysb[b, nh] = yt
+
+        def scatter(b, nh):
+            nc.vector.tensor_tensor(
+                windows[nh][:].indirect(dst_t[:, 8 * b : 8 * (b + 1)]),
+                ysb[b, nh][:],
+                gate_t[:, P * b : P * (b + 1)],
+                MULT,
+            )
 
         quantise(0, 0, P)
-        quantise(0, 1, P)
+        quantise(0, 1, 64)
         gather_words(0, 0, C)
-        gather_scales(0, 0, C)
-        for b in range(2):
-            first_layer(0, b)
-        gather_words(0, C, T)
         quantise(1, 0, HALF)
-        quantise(1, 1, HALF)
-        gather_scales(0, C, T, tag="grouped1_0_0")
-        for b in range(2, 4):
-            first_layer(0, b)
-        gather_words(1, 0, C)
-        gather_scales(1, 0, C)
-        for b in range(2):
-            first_layer(1, b)
-        gather_words(1, C, T)
+        quantise(1, 1, 64)
+        gather_scales01(0, "gs01_0")
+        gather_words(1, 0, P)
         quantise(2, 0, HALF)
-        quantise(2, 1, HALF)
-        gather_scales(1, C, T, tag="grouped2_0_0")
-        for b in range(2, 4):
-            first_layer(1, b)
+        quantise(2, 1, 64)
+        gather_words(2, 0, P)
+        gather_scales2(0, P)
+        gather_words(1, P, C, "grouped2_1")
+        gather_words(2, P, C)
+        gather_scales2(P, C)
         for b in range(2):
-            gather_words(2, P * b, P * (b + 1))
-            gather_scales(2, P * b, P * (b + 1))
-            first_layer(2, b)
-            activate(b)
-            turn(b)
-            regroup(b, P * b, P * (b + 1))
+            for s in ORDERS[b]:
+                first_layer(s, b)
+        hidden(0)
+        hidden(1)
+        late_loads()
+        gather_scales01(C, "raw2_1")
         gather_words(2, C, T)
-        gather_scales(2, C, T)
-        second_layer(0, P, 0)
-        second_layer(P, C, 1)
-        first_layer(2, 2)
-        first_layer(2, 3)
-        scatter(0, P)
+        gather_scales2(C, T)
+        gather_words(1, C, T, "gw1_0")
+        second_layer(0)
+        gather_words(0, C, T, "hgrouped0")
+        leave(0, 0)
+        leave(0, 1)
+        second_layer(1)
+        leave(1, 0)
+        scatter(0, 0)
+        scatter(0, 1)
         for b in range(2, 4):
-            activate(b)
-            turn(b)
-            regroup(b, C, T)
-        second_layer(C, T, 0)
-        scatter(P, C)
-        scatter(C, T)
+            for s in ORDERS[b]:
+                first_layer(s, b)
+        hidden(2)
+        second_layer(2)
+        leave(1, 1, tag="h2")
+        scatter(1, 0)
+        scatter(1, 1)
+        hidden(3)
+        second_layer(3)
+        for b in range(2, 4):
+            for nh in range(2):
+                leave(b, nh)
+                scatter(b, nh)
         for nh in range(2):
             nc.sync.dma_start(out[P * nh : P * (nh + 1), :], windows[nh][:])

@@ -18,7 +18,7 @@ E2M1 = mybir.dt.float4_e2m1fn_x4
 P = 128
 PASSES = K // 512
 HALF = T // 2
-ORDERS = ((1, 0, 2), (0, 1, 2), (2, 1, 0), (2, 1, 0))
+ORDERS = ((1, 0, 2), (1, 0, 2), (0, 2, 1), (0, 2, 1))
 COPY = mybir.ActivationFunctionType.Copy
 SILU = mybir.ActivationFunctionType.Silu
 MULT = mybir.AluOpType.mult
@@ -92,8 +92,8 @@ def tile_moe_two_mlp_silu_kernel(
                     w2_sc[32 * q : 32 * q + 4].bitcast(I32),
                     w2_scales[:, 0, 4 * q : 4 * q + 4, :].rearrange("e q n -> q e n").bitcast(I32),
                 )
-            load_w1(1, 0, PASSES)
             nc.sync.dma_start(w2_t[:], w2_words.rearrange("e s p c -> p (e s) c"))
+            load_w1(1, 0, PASSES)
             nc.sync.dma_start(gate_t[:], gate[0:P, :])
 
         ident = keep.tile([P, P], F32, name="ident")
@@ -222,39 +222,37 @@ def tile_moe_two_mlp_silu_kernel(
         quantise(0, 0, P)
         quantise(0, 1, 64)
         gather_words(0, 0, C)
+        gather_words(0, C, T)
         quantise(1, 0, HALF)
-        quantise(1, 1, 64)
+        quantise(1, 1, P)
         gather_scales01(0, "gs01_0")
-        gather_words(1, 0, P)
+        gather_scales01(C, "gs01_1")
+        late_loads()
+        gather_words(1, 0, C)
         quantise(2, 0, HALF)
-        quantise(2, 1, 64)
-        gather_words(2, 0, P)
-        gather_scales2(0, P)
-        gather_words(1, P, C, "grouped2_1")
-        gather_words(2, P, C)
-        gather_scales2(P, C)
+        quantise(2, 1, HALF)
         for b in range(2):
+            gather_words(2, P * b, P * (b + 1))
+            gather_scales2(P * b, P * (b + 1))
             for s in ORDERS[b]:
                 first_layer(s, b)
         hidden(0)
         hidden(1)
-        late_loads()
-        gather_scales01(C, "raw2_1")
         gather_words(2, C, T)
         gather_scales2(C, T)
-        gather_words(1, C, T, "gw1_0")
+        gather_words(1, C, T, "gw0_0")
         second_layer(0)
-        gather_words(0, C, T, "hgrouped0")
         leave(0, 0)
+        for s in ORDERS[2]:
+            first_layer(s, 2)
+        hidden(2)
         leave(0, 1)
         second_layer(1)
         leave(1, 0)
         scatter(0, 0)
         scatter(0, 1)
-        for b in range(2, 4):
-            for s in ORDERS[b]:
-                first_layer(s, b)
-        hidden(2)
+        for s in ORDERS[3]:
+            first_layer(s, 3)
         second_layer(2)
         leave(1, 1, tag="h2")
         scatter(1, 0)

@@ -137,11 +137,11 @@ def tile_moe_two_mlp_silu_kernel(
             for b in range(c0 // P, c1 // P):
                 gs[2, b] = g[:, P * b - c0 : P * b - c0 + P]
 
-        def gather_scales01(c0, tag):
-            g = keep.tile([P, C], U8, name=f"gs01_{c0}", tag=tag, align_bytes=64)
-            nc.vector.tensor_copy(g[:], scales01[:].indirect(offs_t[:, c0 // 16 : (c0 + C) // 16]))
-            nc.sync.dma_start(moved0[0:100, c0 : c0 + C].bitcast(I32), g[4:104].bitcast(I32))
-            for b in range(c0 // P, (c0 + C) // P):
+        def gather_scales01(c0, c1):
+            g = keep.tile([P, c1 - c0], U8, name=f"gs01_{c0}", align_bytes=64)
+            nc.vector.tensor_copy(g[:], scales01[:].indirect(offs_t[:, c0 // 16 : c1 // 16]))
+            nc.sync.dma_start(moved0[0:100, c0:c1].bitcast(I32), g[4:104].bitcast(I32))
+            for b in range(c0 // P, c1 // P):
                 gs[1, b] = g[:, P * b - c0 : P * b - c0 + P]
                 gs[0, b] = moved0[:, P * b : P * (b + 1)]
 
@@ -222,11 +222,10 @@ def tile_moe_two_mlp_silu_kernel(
         quantise(0, 0, P)
         quantise(0, 1, 64)
         gather_words(0, 0, C)
-        gather_words(0, C, T)
         quantise(1, 0, HALF)
-        quantise(1, 1, P)
-        gather_scales01(0, "gs01_0")
-        gather_scales01(C, "gs01_1")
+        quantise(1, 1, 96)
+        gather_scales01(0, P)
+        gather_scales01(P, T)
         late_loads()
         gather_words(1, 0, C)
         quantise(2, 0, HALF)
@@ -240,6 +239,7 @@ def tile_moe_two_mlp_silu_kernel(
         hidden(1)
         gather_words(2, C, T)
         gather_scales2(C, T)
+        gather_words(0, C, T, "gw2_0")
         gather_words(1, C, T, "gw0_0")
         second_layer(0)
         leave(0, 0)

@@ -18,7 +18,7 @@ E2M1 = mybir.dt.float4_e2m1fn_x4
 P = 128
 PASSES = K // 512
 HALF = T // 2
-ORDERS = ((1, 0, 2), (1, 0, 2), (0, 2, 1), (0, 2, 1))
+ORDER = (1, 0, 2)
 COPY = mybir.ActivationFunctionType.Copy
 SILU = mybir.ActivationFunctionType.Silu
 MULT = mybir.AluOpType.mult
@@ -44,11 +44,11 @@ def tile_moe_two_mlp_silu_kernel(
         w1_sc = keep.tile([P, E * PASSES, H], U8, name="w1_sc", align_bytes=64)
         w2_sc = keep.tile([P, E, N], U8, name="w2_sc", align_bytes=64)
         nc.vector.memset(w1_sc[:].rearrange("p e i -> p (e i)").bitcast(I32), 0)
-        nc.vector.memset(w2_sc[:].rearrange("p e i -> p (e i)").bitcast(I32), 0)
+        nc.gpsimd.memset(w2_sc[:].rearrange("p e i -> p (e i)").bitcast(I32), 0)
 
         scales01 = keep.tile([P, T], U8, name="scales01", align_bytes=64)
         scales2 = keep.tile([P, T], U8, name="scales2", align_bytes=64)
-        moved0 = keep.tile([P, T], U8, name="moved0", align_bytes=64)
+        moved0 = keep.tile([P, C], U8, name="moved0", align_bytes=64)
         for plane in (scales01, scales2, moved0):
             nc.gpsimd.memset(plane[:].bitcast(I32), 0)
         scales = [scales01[4:P], scales01[:], scales2[:]]
@@ -63,38 +63,41 @@ def tile_moe_two_mlp_silu_kernel(
 
         w1_t = {}
 
-        def load_w1(e, s0, s1):
-            tile = keep.tile([P, s1 - s0, 2 * H], U8, name=f"w1_{e}_{s0}", align_bytes=64)
-            nc.sync.dma_start(tile[:], w1_words[e, s0:s1].rearrange("s p c -> p s c"))
-            for s in range(s0, s1):
-                w1_t[e, s] = tile[:, s - s0, :]
+        def load_w1(s):
+            tile = keep.tile([P, E, 2 * H], U8, name=f"w1_{s}", align_bytes=64)
+            nc.sync.dma_start(tile[:], w1_words[:, s].rearrange("e p c -> p e c"))
+            for e in range(E):
+                w1_t[e, s] = tile[:, e, :]
+
+        def w2_scale_rows(q0, q1):
+            for q in range(q0, q1):
+                nc.sync.dma_start(
+                    w2_sc[32 * q : 32 * q + 4].bitcast(I32),
+                    w2_scales[:, 0, 4 * q : 4 * q + 4, :].rearrange("e q n -> q e n").bitcast(I32),
+                )
 
         load_x(0, 0)
-        load_x(0, 1)
         nc.sync.dma_start(offs_t[:], offs)
+        load_x(0, 1)
+        w2_scale_rows(0, 3)
         load_x(1, 0)
         load_x(1, 1)
         load_x(2, 0)
-        load_x(2, 1)
         for q in range(4):
             nc.sync.dma_start(
                 w1_sc[32 * q : 32 * q + 4].bitcast(I32),
                 w1_scales[:, :, 4 * q : 4 * q + 4, :].rearrange("e s q i -> q (e s) i").bitcast(I32),
             )
-        load_w1(0, 0, PASSES)
+        load_w1(1)
+        load_x(2, 1)
+        load_w1(0)
+        load_w1(2)
         w2_t = keep.tile([P, E, 2 * N], U8, name="w2_t", align_bytes=64)
+        w2_scale_rows(3, 4)
+        nc.sync.dma_start(w2_t[:], w2_words.rearrange("e s p c -> p (e s) c"))
+        nc.sync.dma_start(dst_t[:], dst)
         gate_t = keep.tile([P, T], F32, name="gate_t")
-
-        def late_loads():
-            nc.sync.dma_start(dst_t[:], dst)
-            for q in range(4):
-                nc.sync.dma_start(
-                    w2_sc[32 * q : 32 * q + 4].bitcast(I32),
-                    w2_scales[:, 0, 4 * q : 4 * q + 4, :].rearrange("e q n -> q e n").bitcast(I32),
-                )
-            nc.sync.dma_start(w2_t[:], w2_words.rearrange("e s p c -> p (e s) c"))
-            load_w1(1, 0, PASSES)
-            nc.sync.dma_start(gate_t[:], gate[0:P, :])
+        nc.sync.dma_start(gate_t[:], gate[0:P, :])
 
         ident = keep.tile([P, P], F32, name="ident")
         make_identity(nc, ident[:])
@@ -137,19 +140,21 @@ def tile_moe_two_mlp_silu_kernel(
             for b in range(c0 // P, c1 // P):
                 gs[2, b] = g[:, P * b - c0 : P * b - c0 + P]
 
-        def gather_scales01(c0, c1):
+        def gather_scales01(c0, c1, moved):
             g = keep.tile([P, c1 - c0], U8, name=f"gs01_{c0}", align_bytes=64)
             nc.vector.tensor_copy(g[:], scales01[:].indirect(offs_t[:, c0 // 16 : c1 // 16]))
-            nc.sync.dma_start(moved0[0:100, c0:c1].bitcast(I32), g[4:104].bitcast(I32))
+            if moved is None:
+                moved = keep.tile([P, c1 - c0], U8, name="moved1", tag="raw2_0", align_bytes=64)
+            nc.sync.dma_start(moved[0:100].bitcast(I32), g[4:104].bitcast(I32))
             for b in range(c0 // P, c1 // P):
                 gs[1, b] = g[:, P * b - c0 : P * b - c0 + P]
-                gs[0, b] = moved0[:, P * b : P * (b + 1)]
+                gs[0, b] = moved[:, P * b - c0 : P * b - c0 + P]
 
         acc = {}
 
         def first_layer(s, b):
             e = b // 2
-            if s == ORDERS[b][0]:
+            if s == ORDER[0]:
                 acc[b] = psum.tile([P, H], F32, name=f"acc{b}", tag=f"bank{b}")
             nc.tensor.matmul_mx(
                 out=acc[b][:],
@@ -157,8 +162,8 @@ def tile_moe_two_mlp_silu_kernel(
                 lhsT_scale=gs[s, b],
                 rhs=w1_t[e, s].bitcast(E2M1),
                 rhs_scale=w1_sc[:, e * PASSES + s, :],
-                start=(s == ORDERS[b][0]),
-                stop=(s == ORDERS[b][-1]),
+                start=(s == ORDER[0]),
+                stop=(s == ORDER[-1]),
             )
 
         grouped_h = {}
@@ -174,14 +179,18 @@ def tile_moe_two_mlp_silu_kernel(
             )
             h_pairs = h[:].bitcast(F32)
             h_t[b] = h
-            turned = psum.tile([P, 2, P], F32, name=f"turned{b}", tag=f"bank{(b + 2) % 4}")
+            turned = psum.tile([P, 2, P], F32, name=f"turned{b}", tag=f"turned{b}" if b < 2 else f"bank{b - 2}")
             for u in range(2):
                 nc.tensor.transpose(turned[:, u, :], h_pairs[:, P * u : P * (u + 1)], ident[:])
             grouped_h[b] = keep.tile([P, P, 4], BF16, name=f"hgrouped{b}", tag=f"hgrouped{b}", align_bytes=64)
             pairs = grouped_h[b][:].rearrange("p r f -> p (r f)").bitcast(F32).rearrange("p (r u) -> p r u", u=2)
-            nc.scalar.copy(pairs, turned[:].rearrange("p u r -> p r u"))
+            if b == 0:
+                nc.vector.tensor_copy(pairs, turned[:].rearrange("p u r -> p r u"))
+            else:
+                nc.scalar.copy(pairs, turned[:].rearrange("p u r -> p r u"))
 
-        windows = [keep.tile([P, T], F32, name=f"window{nh}") for nh in range(2)]
+        windows = {}
+
         y = {}
         ysb = {}
 
@@ -193,10 +202,15 @@ def tile_moe_two_mlp_silu_kernel(
                 out=hw[:].bitcast(E4M3), scales=hsc[:], in_=grouped_h[b][:].rearrange("p r f -> p (r f)")
             )
             hw_t[b] = hw
-            y[b] = psum.tile([P, 2, P], F32, name=f"y{b}")
+            if b < 3:
+                y[b] = psum.tile([P, 2, P], F32, name=f"y{b}", tag=f"y{b}" if b < 2 else "turned0")
+                sums = [y[b][:, nh, :] for nh in range(2)]
+            else:
+                y[b] = [psum.tile([P, P], F32, name=f"y3_{nh}", tag=("turned1", "y0")[nh]) for nh in range(2)]
+                sums = [y[b][nh][:] for nh in range(2)]
             for nh in range(2):
                 nc.tensor.matmul_mx(
-                    out=y[b][:, nh, :],
+                    out=sums[nh],
                     lhsT=w2_t[:, e, N * nh : N * (nh + 1)].bitcast(E2M1),
                     lhsT_scale=w2_sc[:, e, P * nh : P * (nh + 1)],
                     rhs=hw[:].bitcast(E4M3),
@@ -205,63 +219,64 @@ def tile_moe_two_mlp_silu_kernel(
                     stop=True,
                 )
 
-        def leave(b, nh, tag=None):
-            name = f"ysb{b}_{nh}"
-            yt = keep.tile([P, P], F32, name=name, tag=name if tag is None else tag)
-            nc.scalar.activation(yt[:], y[b][:, nh, :], COPY)
-            ysb[b, nh] = yt
+        gated = keep.tile([P, 2, T], F32, name="gated")
 
-        def scatter(b, nh):
+        def leave(b):
             nc.vector.tensor_tensor(
-                windows[nh][:].indirect(dst_t[:, 8 * b : 8 * (b + 1)]),
-                ysb[b, nh][:],
-                gate_t[:, P * b : P * (b + 1)],
+                gated[:, :, P * b : P * (b + 1)],
+                y[b][:],
+                gate_t[:, P * b : P * (b + 1)].unsqueeze(1).broadcast_to([P, 2, P]),
                 MULT,
             )
 
+        def scatter(engine, nh, c0, c1):
+            places = dst_t[:, c0 // 16 : c1 // 16]
+            if engine is nc.scalar:
+                nc.scalar.activation(windows[nh][:].indirect(places), gated[:, nh, c0:c1], COPY)
+            else:
+                nc.vector.tensor_copy(windows[nh][:].indirect(places), gated[:, nh, c0:c1])
+
         quantise(0, 0, P)
-        quantise(0, 1, 64)
+        quantise(0, 1, P)
         gather_words(0, 0, C)
+        gather_words(0, C, T)
         quantise(1, 0, HALF)
-        quantise(1, 1, 96)
-        gather_scales01(0, P)
-        gather_scales01(P, T)
-        late_loads()
+        quantise(1, 1, P)
+        gather_scales01(0, C, moved0)
         gather_words(1, 0, C)
         quantise(2, 0, HALF)
+        gather_scales01(C, T, None)
+        gather_words(1, C, T)
         quantise(2, 1, HALF)
-        for b in range(2):
+        for b in range(4):
             gather_words(2, P * b, P * (b + 1))
             gather_scales2(P * b, P * (b + 1))
-            for s in ORDERS[b]:
-                first_layer(s, b)
-        hidden(0)
-        hidden(1)
-        gather_words(2, C, T)
-        gather_scales2(C, T)
-        gather_words(0, C, T, "gw2_0")
-        gather_words(1, C, T, "gw0_0")
+        for b in range(4):
+            first_layer(ORDER[0], b)
+        for e in range(E):
+            for s in ORDER[1:]:
+                for b in range(2 * e, 2 * e + 2):
+                    first_layer(s, b)
+            if e == 0:
+                hidden(0)
+                hidden(1)
         second_layer(0)
-        leave(0, 0)
-        for s in ORDERS[2]:
-            first_layer(s, 2)
-        hidden(2)
-        leave(0, 1)
         second_layer(1)
-        leave(1, 0)
-        scatter(0, 0)
-        scatter(0, 1)
-        for s in ORDERS[3]:
-            first_layer(s, 3)
-        second_layer(2)
-        leave(1, 1, tag="h2")
-        scatter(1, 0)
-        scatter(1, 1)
+        hidden(2)
         hidden(3)
+        leave(0)
+        leave(1)
+        second_layer(2)
         second_layer(3)
-        for b in range(2, 4):
-            for nh in range(2):
-                leave(b, nh)
-                scatter(b, nh)
+        windows[0] = keep.tile([P, T], F32, name="window0", tag="hgrouped2", align_bytes=64)
+        windows[1] = keep.tile([P, T], F32, name="window1")
+        leave(2)
         for nh in range(2):
-            nc.sync.dma_start(out[P * nh : P * (nh + 1), :], windows[nh][:])
+            nc.vector.tensor_tensor(gated[:, nh, 3 * P : T], y[3][nh][:], gate_t[:, 3 * P : T], MULT)
+        scatter(nc.vector, 1, 0, 64)
+        scatter(nc.scalar, 0, 0, P)
+        scatter(nc.scalar, 1, 64, C)
+        scatter(nc.scalar, 1, C, T)
+        scatter(nc.vector, 0, P, T)
+        nc.scalar.dma_start(out[P : 2 * P, :], windows[1][:])
+        nc.sync.dma_start(out[0:P, :], windows[0][:])

@@ -48,7 +48,7 @@ def tile_moe_two_mlp_silu_kernel(
 
         scales01 = keep.tile([P, T], U8, name="scales01", align_bytes=64)
         scales2 = keep.tile([P, T], U8, name="scales2", align_bytes=64)
-        moved0 = keep.tile([P, C], U8, name="moved0", align_bytes=64)
+        moved0 = keep.tile([P, T], U8, name="moved0", align_bytes=64)
         for plane in (scales01, scales2, moved0):
             nc.gpsimd.memset(plane[:].bitcast(I32), 0)
         scales = [scales01[4:P], scales01[:], scales2[:]]
@@ -83,21 +83,19 @@ def tile_moe_two_mlp_silu_kernel(
         load_x(1, 0)
         load_x(1, 1)
         load_x(2, 0)
+        load_x(2, 1)
         for q in range(4):
             nc.sync.dma_start(
                 w1_sc[32 * q : 32 * q + 4].bitcast(I32),
                 w1_scales[:, :, 4 * q : 4 * q + 4, :].rearrange("e s q i -> q (e s) i").bitcast(I32),
             )
         load_w1(1)
-        load_x(2, 1)
         load_w1(0)
         load_w1(2)
         w2_t = keep.tile([P, E, 2 * N], U8, name="w2_t", align_bytes=64)
         w2_scale_rows(3, 4)
         nc.sync.dma_start(w2_t[:], w2_words.rearrange("e s p c -> p (e s) c"))
         nc.sync.dma_start(dst_t[:], dst)
-        gate_t = keep.tile([P, T], F32, name="gate_t")
-        nc.sync.dma_start(gate_t[:], gate[0:P, :])
 
         ident = keep.tile([P, P], F32, name="ident")
         make_identity(nc, ident[:])
@@ -140,15 +138,13 @@ def tile_moe_two_mlp_silu_kernel(
             for b in range(c0 // P, c1 // P):
                 gs[2, b] = g[:, P * b - c0 : P * b - c0 + P]
 
-        def gather_scales01(c0, c1, moved):
+        def gather_scales01(c0, c1):
             g = keep.tile([P, c1 - c0], U8, name=f"gs01_{c0}", align_bytes=64)
             nc.vector.tensor_copy(g[:], scales01[:].indirect(offs_t[:, c0 // 16 : c1 // 16]))
-            if moved is None:
-                moved = keep.tile([P, c1 - c0], U8, name="moved1", tag="raw2_0", align_bytes=64)
-            nc.sync.dma_start(moved[0:100].bitcast(I32), g[4:104].bitcast(I32))
+            nc.sync.dma_start(moved0[0:100, c0:c1].bitcast(I32), g[4:104].bitcast(I32))
             for b in range(c0 // P, c1 // P):
                 gs[1, b] = g[:, P * b - c0 : P * b - c0 + P]
-                gs[0, b] = moved[:, P * b - c0 : P * b - c0 + P]
+                gs[0, b] = moved0[:, P * b : P * (b + 1)]
 
         acc = {}
 
@@ -242,11 +238,12 @@ def tile_moe_two_mlp_silu_kernel(
         gather_words(0, C, T)
         quantise(1, 0, HALF)
         quantise(1, 1, P)
-        gather_scales01(0, C, moved0)
-        gather_words(1, 0, C)
+        for c0 in (0, C):
+            gather_scales01(c0, c0 + C)
+            gather_words(1, c0, c0 + C)
         quantise(2, 0, HALF)
-        gather_scales01(C, T, None)
-        gather_words(1, C, T)
+        gate_t = keep.tile([P, T], F32, name="gate_t", tag="raw2_0", align_bytes=64)
+        nc.sync.dma_start(gate_t[:], gate[0:P, :])
         quantise(2, 1, HALF)
         for b in range(4):
             gather_words(2, P * b, P * (b + 1))

@@ -79,7 +79,6 @@ def tile_moe_two_mlp_silu_kernel(
         load_x(0, 0)
         nc.sync.dma_start(offs_t[:], offs)
         load_x(0, 1)
-        w2_scale_rows(0, 3)
         load_x(1, 0)
         load_x(1, 1)
         load_x(2, 0)
@@ -92,10 +91,6 @@ def tile_moe_two_mlp_silu_kernel(
         load_w1(1)
         load_w1(0)
         load_w1(2)
-        w2_t = keep.tile([P, E, 2 * N], U8, name="w2_t", align_bytes=64)
-        w2_scale_rows(3, 4)
-        nc.sync.dma_start(w2_t[:], w2_words.rearrange("e s p c -> p (e s) c"))
-        nc.sync.dma_start(dst_t[:], dst)
 
         ident = keep.tile([P, P], F32, name="ident")
         make_identity(nc, ident[:])
@@ -241,9 +236,13 @@ def tile_moe_two_mlp_silu_kernel(
         for c0 in (0, C):
             gather_scales01(c0, c0 + C)
             gather_words(1, c0, c0 + C)
-        quantise(2, 0, HALF)
-        gate_t = keep.tile([P, T], F32, name="gate_t", tag="raw2_0", align_bytes=64)
+        w2_t = keep.tile([P, E, 2 * N], U8, name="w2_t", align_bytes=64)
+        w2_scale_rows(0, 4)
+        nc.sync.dma_start(w2_t[:], w2_words.rearrange("e s p c -> p (e s) c"))
+        gate_t = keep.tile([P, T], F32, name="gate_t")
         nc.sync.dma_start(gate_t[:], gate[0:P, :])
+        nc.sync.dma_start(dst_t[:], dst)
+        quantise(2, 0, HALF)
         quantise(2, 1, HALF)
         for b in range(4):
             gather_words(2, P * b, P * (b + 1))

@@ -14,14 +14,20 @@ U16 = mybir.dt.uint16
 U8 = mybir.dt.uint8
 E4M3 = mybir.dt.float8_e4m3fn_x4
 E2M1 = mybir.dt.float4_e2m1fn_x4
-
-P = 128
-PASSES = K // 512
-HALF = T // 2
-ORDER = (1, 0, 2)
 COPY = mybir.ActivationFunctionType.Copy
 SILU = mybir.ActivationFunctionType.Silu
 MULT = mybir.AluOpType.mult
+
+P = 128
+PASSES = K // 512
+TILES = E * C // P
+LAST_TILE = TILES - 1
+HALF = T // 2
+QUADRANTS = 4
+SHIFT = 4
+PLANE_ROWS = 100
+PASS_ORDER = (1, 0, 2)
+EARLY_COLUMNS = 64
 
 
 def interleave_views(dst, src):
@@ -51,7 +57,7 @@ def tile_moe_two_mlp_silu_kernel(
         moved0 = keep.tile([P, T], U8, name="moved0", align_bytes=64)
         for plane in (scales01, scales2, moved0):
             nc.gpsimd.memset(plane[:].bitcast(I32), 0)
-        scales = [scales01[4:P], scales01[:], scales2[:]]
+        scales = [scales01[SHIFT:P], scales01[:], scales2[:]]
 
         raw = {}
 
@@ -69,28 +75,20 @@ def tile_moe_two_mlp_silu_kernel(
             for e in range(E):
                 w1_t[e, s] = tile[:, e, :]
 
-        def w2_scale_rows(q0, q1):
-            for q in range(q0, q1):
-                nc.sync.dma_start(
-                    w2_sc[32 * q : 32 * q + 4].bitcast(I32),
-                    w2_scales[:, 0, 4 * q : 4 * q + 4, :].rearrange("e q n -> q e n").bitcast(I32),
-                )
-
         load_x(0, 0)
         nc.sync.dma_start(offs_t[:], offs)
+        nc.sync.dma_start(dst_t[:], dst)
         load_x(0, 1)
-        load_x(1, 0)
-        load_x(1, 1)
-        load_x(2, 0)
-        load_x(2, 1)
-        for q in range(4):
+        for s in range(1, PASSES):
+            for half in range(2):
+                load_x(s, half)
+        for q in range(QUADRANTS):
             nc.sync.dma_start(
                 w1_sc[32 * q : 32 * q + 4].bitcast(I32),
                 w1_scales[:, :, 4 * q : 4 * q + 4, :].rearrange("e s q i -> q (e s) i").bitcast(I32),
             )
-        load_w1(1)
-        load_w1(0)
-        load_w1(2)
+        for s in PASS_ORDER:
+            load_w1(s)
 
         ident = keep.tile([P, P], F32, name="ident")
         make_identity(nc, ident[:])
@@ -100,19 +98,16 @@ def tile_moe_two_mlp_silu_kernel(
         nc.scalar.activation(warm_out[:], warm[:], SILU)
 
         words = [keep.tile([P, T], U32, name=f"words{s}", align_bytes=64) for s in range(PASSES)]
-        gw = {}
-        gs = {}
+        slot_words = {}
+        slot_scales = {}
 
-        def quantise(s, half, vector_from):
+        def quantise(s, half, on_scalar):
             grouped = keep.tile([P, HALF, 4], BF16, name=f"grouped{s}_{half}", tag=f"grouped{s}_{half}", align_bytes=64)
-            for engine, t0, t1 in [(nc.scalar, 0, vector_from), (nc.vector, vector_from, HALF)]:
-                if t0 == t1:
-                    continue
-                to, frm = interleave_views(grouped[:, t0:t1, :], raw[s, half][:, :, t0:t1])
-                if engine is nc.scalar:
-                    nc.scalar.activation(to, frm, COPY)
-                else:
-                    nc.vector.tensor_copy(to, frm)
+            to, frm = interleave_views(grouped[:, 0:on_scalar, :], raw[s, half][:, :, 0:on_scalar])
+            nc.scalar.activation(to, frm, COPY)
+            if on_scalar < HALF:
+                to, frm = interleave_views(grouped[:, on_scalar:HALF, :], raw[s, half][:, :, on_scalar:HALF])
+                nc.vector.tensor_copy(to, frm)
             cols = slice(HALF * half, HALF * (half + 1))
             nc.vector.quantize_mx(
                 out=words[s][:, cols].bitcast(E4M3),
@@ -120,46 +115,45 @@ def tile_moe_two_mlp_silu_kernel(
                 in_=grouped[:].rearrange("p t j -> p (t j)"),
             )
 
-        def gather_words(s, c0, c1, tag=None):
-            name = f"gw{s}_{c0}"
-            w = keep.tile([P, c1 - c0], U32, name=name, tag=name if tag is None else tag, align_bytes=64)
-            nc.vector.tensor_copy(w[:], words[s][:].indirect(offs_t[:, c0 // 16 : c1 // 16]))
+        def gather_words(s, c0, c1):
+            gathered = keep.tile([P, c1 - c0], U32, name=f"gw{s}_{c0}", tag=f"gw{s}_{c0}", align_bytes=64)
+            nc.vector.tensor_copy(gathered[:], words[s][:].indirect(offs_t[:, c0 // 16 : c1 // 16]))
             for b in range(c0 // P, c1 // P):
-                gw[s, b] = w[:, P * b - c0 : P * b - c0 + P]
+                slot_words[s, b] = gathered[:, P * b - c0 : P * b - c0 + P]
 
-        def gather_scales2(c0, c1):
-            g = keep.tile([P, c1 - c0], U8, name=f"gs2_{c0}", align_bytes=64)
-            nc.vector.tensor_copy(g[:], scales2[:].indirect(offs_t[:, c0 // 16 : c1 // 16]))
-            for b in range(c0 // P, c1 // P):
-                gs[2, b] = g[:, P * b - c0 : P * b - c0 + P]
+        def gather_scales2(b):
+            gathered = keep.tile([P, P], U8, name=f"gs2_{P * b}", align_bytes=64)
+            nc.vector.tensor_copy(gathered[:], scales2[:].indirect(offs_t[:, P * b // 16 : P * (b + 1) // 16]))
+            slot_scales[2, b] = gathered[:, 0:P]
 
-        def gather_scales01(c0, c1):
-            g = keep.tile([P, c1 - c0], U8, name=f"gs01_{c0}", align_bytes=64)
-            nc.vector.tensor_copy(g[:], scales01[:].indirect(offs_t[:, c0 // 16 : c1 // 16]))
-            nc.sync.dma_start(moved0[0:100, c0:c1].bitcast(I32), g[4:104].bitcast(I32))
+        def gather_scales01(e):
+            c0, c1 = C * e, C * (e + 1)
+            gathered = keep.tile([P, C], U8, name=f"gs01_{c0}", align_bytes=64)
+            nc.vector.tensor_copy(gathered[:], scales01[:].indirect(offs_t[:, c0 // 16 : c1 // 16]))
+            nc.sync.dma_start(
+                moved0[0:PLANE_ROWS, c0:c1].bitcast(I32), gathered[SHIFT : SHIFT + PLANE_ROWS].bitcast(I32)
+            )
             for b in range(c0 // P, c1 // P):
-                gs[1, b] = g[:, P * b - c0 : P * b - c0 + P]
-                gs[0, b] = moved0[:, P * b : P * (b + 1)]
+                slot_scales[1, b] = gathered[:, P * b - c0 : P * b - c0 + P]
+                slot_scales[0, b] = moved0[:, P * b : P * (b + 1)]
 
         acc = {}
 
         def first_layer(s, b):
             e = b // 2
-            if s == ORDER[0]:
+            if s == PASS_ORDER[0]:
                 acc[b] = psum.tile([P, H], F32, name=f"acc{b}", tag=f"bank{b}")
             nc.tensor.matmul_mx(
                 out=acc[b][:],
-                lhsT=gw[s, b].bitcast(E4M3),
-                lhsT_scale=gs[s, b],
+                lhsT=slot_words[s, b].bitcast(E4M3),
+                lhsT_scale=slot_scales[s, b],
                 rhs=w1_t[e, s].bitcast(E2M1),
                 rhs_scale=w1_sc[:, e * PASSES + s, :],
-                start=(s == ORDER[0]),
-                stop=(s == ORDER[-1]),
+                start=(s == PASS_ORDER[0]),
+                stop=(s == PASS_ORDER[-1]),
             )
 
         grouped_h = {}
-        h_t = {}
-        hw_t = {}
 
         def hidden(b):
             h = keep.tile([P, H], BF16, name=f"h{b}", tag=f"h{b}")
@@ -169,7 +163,6 @@ def tile_moe_two_mlp_silu_kernel(
                 SILU,
             )
             h_pairs = h[:].bitcast(F32)
-            h_t[b] = h
             turned = psum.tile([P, 2, P], F32, name=f"turned{b}", tag=f"turned{b}" if b < 2 else f"bank{b - 2}")
             for u in range(2):
                 nc.tensor.transpose(turned[:, u, :], h_pairs[:, P * u : P * (u + 1)], ident[:])
@@ -180,20 +173,16 @@ def tile_moe_two_mlp_silu_kernel(
             else:
                 nc.scalar.copy(pairs, turned[:].rearrange("p u r -> p r u"))
 
-        windows = {}
-
         y = {}
-        ysb = {}
 
         def second_layer(b):
             e = b // 2
-            hw = keep.tile([P, P], U32, name=f"hw{b}", align_bytes=64)
-            hsc = keep.tile([P, P], U8, name=f"hsc{b}", tag=f"hsc{b}", align_bytes=64)
+            h_words = keep.tile([P, P], U32, name=f"hw{b}", align_bytes=64)
+            h_scales = keep.tile([P, P], U8, name=f"hsc{b}", tag=f"hsc{b}", align_bytes=64)
             nc.vector.quantize_mx(
-                out=hw[:].bitcast(E4M3), scales=hsc[:], in_=grouped_h[b][:].rearrange("p r f -> p (r f)")
+                out=h_words[:].bitcast(E4M3), scales=h_scales[:], in_=grouped_h[b][:].rearrange("p r f -> p (r f)")
             )
-            hw_t[b] = hw
-            if b < 3:
+            if b < LAST_TILE:
                 y[b] = psum.tile([P, 2, P], F32, name=f"y{b}", tag=f"y{b}" if b < 2 else "turned0")
                 sums = [y[b][:, nh, :] for nh in range(2)]
             else:
@@ -204,15 +193,15 @@ def tile_moe_two_mlp_silu_kernel(
                     out=sums[nh],
                     lhsT=w2_t[:, e, N * nh : N * (nh + 1)].bitcast(E2M1),
                     lhsT_scale=w2_sc[:, e, P * nh : P * (nh + 1)],
-                    rhs=hw[:].bitcast(E4M3),
-                    rhs_scale=hsc[:],
+                    rhs=h_words[:].bitcast(E4M3),
+                    rhs_scale=h_scales[:],
                     start=True,
                     stop=True,
                 )
 
         gated = keep.tile([P, 2, T], F32, name="gated")
 
-        def leave(b):
+        def times_gate(b):
             nc.vector.tensor_tensor(
                 gated[:, :, P * b : P * (b + 1)],
                 y[b][:],
@@ -220,59 +209,68 @@ def tile_moe_two_mlp_silu_kernel(
                 MULT,
             )
 
-        def scatter(engine, nh, c0, c1):
-            places = dst_t[:, c0 // 16 : c1 // 16]
-            if engine is nc.scalar:
-                nc.scalar.activation(windows[nh][:].indirect(places), gated[:, nh, c0:c1], COPY)
-            else:
-                nc.vector.tensor_copy(windows[nh][:].indirect(places), gated[:, nh, c0:c1])
+        placed = {}
 
-        quantise(0, 0, P)
-        quantise(0, 1, P)
-        gather_words(0, 0, C)
-        gather_words(0, C, T)
+        def scatter_on_scalar(nh, c0, c1):
+            nc.scalar.activation(placed[nh][:].indirect(dst_t[:, c0 // 16 : c1 // 16]), gated[:, nh, c0:c1], COPY)
+
+        def scatter_on_vector(nh, c0, c1):
+            nc.vector.tensor_copy(placed[nh][:].indirect(dst_t[:, c0 // 16 : c1 // 16]), gated[:, nh, c0:c1])
+
+        quantise(0, 0, HALF // 2)
+        quantise(0, 1, HALF // 2)
+        for e in range(E):
+            gather_words(0, C * e, C * (e + 1))
         quantise(1, 0, HALF)
-        quantise(1, 1, P)
-        for c0 in (0, C):
-            gather_scales01(c0, c0 + C)
-            gather_words(1, c0, c0 + C)
+        quantise(1, 1, HALF // 2)
+        for e in range(E):
+            gather_scales01(e)
+            gather_words(1, C * e, C * (e + 1))
         w2_t = keep.tile([P, E, 2 * N], U8, name="w2_t", align_bytes=64)
-        w2_scale_rows(0, 4)
+        for q in range(QUADRANTS):
+            nc.sync.dma_start(
+                w2_sc[32 * q : 32 * q + 4].bitcast(I32),
+                w2_scales[:, 0, 4 * q : 4 * q + 4, :].rearrange("e q n -> q e n").bitcast(I32),
+            )
         nc.sync.dma_start(w2_t[:], w2_words.rearrange("e s p c -> p (e s) c"))
         gate_t = keep.tile([P, T], F32, name="gate_t")
         nc.sync.dma_start(gate_t[:], gate[0:P, :])
-        nc.sync.dma_start(dst_t[:], dst)
         quantise(2, 0, HALF)
         quantise(2, 1, HALF)
-        for b in range(4):
+        for b in range(TILES):
             gather_words(2, P * b, P * (b + 1))
-            gather_scales2(P * b, P * (b + 1))
-        for b in range(4):
-            first_layer(ORDER[0], b)
-        for e in range(E):
-            for s in ORDER[1:]:
-                for b in range(2 * e, 2 * e + 2):
-                    first_layer(s, b)
-            if e == 0:
-                hidden(0)
-                hidden(1)
+            gather_scales2(b)
+
+        for b in range(TILES):
+            first_layer(PASS_ORDER[0], b)
+        for s in PASS_ORDER[1:]:
+            for b in (0, 1):
+                first_layer(s, b)
+        hidden(0)
+        hidden(1)
+        for s in PASS_ORDER[1:]:
+            for b in (2, 3):
+                first_layer(s, b)
         second_layer(0)
         second_layer(1)
         hidden(2)
         hidden(3)
-        leave(0)
-        leave(1)
+        times_gate(0)
+        times_gate(1)
         second_layer(2)
         second_layer(3)
-        windows[0] = keep.tile([P, T], F32, name="window0", tag="hgrouped2", align_bytes=64)
-        windows[1] = keep.tile([P, T], F32, name="window1")
-        leave(2)
+        placed[0] = keep.tile([P, T], F32, name="window0", tag="hgrouped2", align_bytes=64)
+        placed[1] = keep.tile([P, T], F32, name="window1")
+        times_gate(2)
         for nh in range(2):
-            nc.vector.tensor_tensor(gated[:, nh, 3 * P : T], y[3][nh][:], gate_t[:, 3 * P : T], MULT)
-        scatter(nc.vector, 1, 0, 64)
-        scatter(nc.scalar, 0, 0, P)
-        scatter(nc.scalar, 1, 64, C)
-        scatter(nc.scalar, 1, C, T)
-        scatter(nc.vector, 0, P, T)
-        nc.scalar.dma_start(out[P : 2 * P, :], windows[1][:])
-        nc.sync.dma_start(out[0:P, :], windows[0][:])
+            nc.vector.tensor_tensor(
+                gated[:, nh, P * LAST_TILE : T], y[LAST_TILE][nh][:], gate_t[:, P * LAST_TILE : T], MULT
+            )
+
+        scatter_on_vector(1, 0, EARLY_COLUMNS)
+        scatter_on_scalar(0, 0, P)
+        scatter_on_scalar(1, EARLY_COLUMNS, C)
+        scatter_on_scalar(1, C, T)
+        scatter_on_vector(0, P, T)
+        nc.scalar.dma_start(out[P : 2 * P, :], placed[1][:])
+        nc.sync.dma_start(out[0:P, :], placed[0][:])

@@ -61,11 +61,12 @@ def tile_moe_two_mlp_silu_kernel(
 
         raw = {}
 
-        def load_x(s, half):
+        def load_x(s):
             rows = xT[512 * s : 512 * (s + 1), :].rearrange("(p j) t -> p j t", j=4)
-            tile = keep.tile([P, 4, HALF], F32, name=f"raw{s}_{half}", tag=f"raw{s}_{half}", align_bytes=64)
-            nc.sync.dma_start(tile[:], rows[:, :, HALF * half : HALF * (half + 1)])
-            raw[s, half] = tile
+            tile = keep.tile([P, 4, T], F32, name=f"raw{s}", tag=f"raw{s}", align_bytes=64)
+            nc.sync.dma_start(tile[:], rows)
+            for half in range(2):
+                raw[s, half] = tile[:, :, HALF * half : HALF * (half + 1)]
 
         w1_t = {}
 
@@ -75,13 +76,11 @@ def tile_moe_two_mlp_silu_kernel(
             for e in range(E):
                 w1_t[e, s] = tile[:, e, :]
 
-        load_x(0, 0)
+        load_x(0)
         nc.sync.dma_start(offs_t[:], offs)
         nc.sync.dma_start(dst_t[:], dst)
-        load_x(0, 1)
         for s in range(1, PASSES):
-            for half in range(2):
-                load_x(s, half)
+            load_x(s)
         for q in range(QUADRANTS):
             nc.sync.dma_start(
                 w1_sc[32 * q : 32 * q + 4].bitcast(I32),

@@ -21,13 +21,11 @@ MULT = mybir.AluOpType.mult
 P = 128
 PASSES = K // 512
 TILES = E * C // P
-LAST_TILE = TILES - 1
 HALF = T // 2
-QUADRANTS = 4
+ROWS = 4
 SHIFT = 4
 PLANE_ROWS = 100
 PASS_ORDER = (1, 0, 2)
-EARLY_COLUMNS = 64
 
 
 def interleave_views(dst, src):
@@ -43,51 +41,50 @@ def tile_moe_two_mlp_silu_kernel(
     nc = tc.nc
     with ExitStack() as ctx:
         keep = ctx.enter_context(tc.tile_pool(name="keep", bufs=1))
+        shared = ctx.enter_context(tc.tile_pool(name="shared", bufs=1))
+        late = ctx.enter_context(tc.tile_pool(name="late", bufs=1))
         psum = ctx.enter_context(tc.psum_pool(name="psum", bufs=1))
 
         offs_t = keep.tile([P, T // 16], U16, name="offs_t")
         dst_t = keep.tile([P, T // 16], U16, name="dst_t")
         w1_sc = keep.tile([P, E * PASSES, H], U8, name="w1_sc", align_bytes=64)
-        w2_sc = keep.tile([P, E, N], U8, name="w2_sc", align_bytes=64)
         nc.vector.memset(w1_sc[:].rearrange("p e i -> p (e i)").bitcast(I32), 0)
+        w2_sc = keep.tile([P, E, N], U8, name="w2_sc", align_bytes=64)
         nc.gpsimd.memset(w2_sc[:].rearrange("p e i -> p (e i)").bitcast(I32), 0)
-
-        scales01 = keep.tile([P, T], U8, name="scales01", align_bytes=64)
-        scales2 = keep.tile([P, T], U8, name="scales2", align_bytes=64)
-        moved0 = keep.tile([P, T], U8, name="moved0", align_bytes=64)
-        for plane in (scales01, scales2, moved0):
+        plane01 = keep.tile([P, T], U8, name="plane01", tag="plane01", align_bytes=64)
+        plane2 = keep.tile([P, T], U8, name="plane2", align_bytes=64)
+        moved = [keep.tile([P, C], U8, name=f"moved{e}", align_bytes=64) for e in range(E)]
+        for plane in (plane01, plane2, *moved):
             nc.gpsimd.memset(plane[:].bitcast(I32), 0)
-        scales = [scales01[SHIFT:P], scales01[:], scales2[:]]
+        planes = [plane01[SHIFT:P], plane01[:], plane2[:]]
 
         raw = {}
 
         def load_x(s):
-            rows = xT[512 * s : 512 * (s + 1), :].rearrange("(p j) t -> p j t", j=4)
-            tile = keep.tile([P, 4, T], F32, name=f"raw{s}", tag=f"raw{s}", align_bytes=64)
-            nc.sync.dma_start(tile[:], rows)
-            for half in range(2):
-                raw[s, half] = tile[:, :, HALF * half : HALF * (half + 1)]
+            raw[s] = keep.tile([P, 4, T], F32, name=f"raw{s}", align_bytes=64)
+            nc.sync.dma_start(raw[s][:], xT[512 * s : 512 * (s + 1), :].rearrange("(p j) t -> p j t", j=4))
 
-        w1_t = {}
-
-        def load_w1(s):
-            tile = keep.tile([P, E, 2 * H], U8, name=f"w1_{s}", align_bytes=64)
-            nc.sync.dma_start(tile[:], w1_words[:, s].rearrange("e p c -> p e c"))
-            for e in range(E):
-                w1_t[e, s] = tile[:, e, :]
-
-        load_x(0)
+        first = []
+        for u in range(2):
+            first.append(keep.tile([P, 2, T], F32, name=f"first{u}", align_bytes=64))
+            nc.sync.dma_start(first[u][:], xT[0:512, :].rearrange("(p j) t -> p j t", j=4)[:, 2 * u : 2 * u + 2, :])
         nc.sync.dma_start(offs_t[:], offs)
-        nc.sync.dma_start(dst_t[:], dst)
-        for s in range(1, PASSES):
-            load_x(s)
-        for q in range(QUADRANTS):
+        for r in range(ROWS):
             nc.sync.dma_start(
-                w1_sc[32 * q : 32 * q + 4].bitcast(I32),
-                w1_scales[:, :, 4 * q : 4 * q + 4, :].rearrange("e s q i -> q (e s) i").bitcast(I32),
+                w2_sc[r:P:32].bitcast(I32),
+                w2_scales[:, 0, r:16:4, :].rearrange("e q n -> q e n").bitcast(I32),
             )
+        load_x(1)
+        load_x(2)
+        for r in range(ROWS):
+            nc.sync.dma_start(
+                w1_sc[r:P:32].bitcast(I32),
+                w1_scales[:, :, r:16:4, :].rearrange("e s q i -> q (e s) i").bitcast(I32),
+            )
+        w1_t = {}
         for s in PASS_ORDER:
-            load_w1(s)
+            w1_t[s] = keep.tile([P, E, 2 * H], U8, name=f"w1_{s}", align_bytes=64)
+            nc.sync.dma_start(w1_t[s][:], w1_words[:, s].rearrange("e p c -> p e c"))
 
         ident = keep.tile([P, P], F32, name="ident")
         make_identity(nc, ident[:])
@@ -96,45 +93,64 @@ def tile_moe_two_mlp_silu_kernel(
         warm_out = keep.tile([P, 1], F32, name="warm_out")
         nc.scalar.activation(warm_out[:], warm[:], SILU)
 
-        words = [keep.tile([P, T], U32, name=f"words{s}", align_bytes=64) for s in range(PASSES)]
+        words = {s: keep.tile([P, T], U32, name=f"words{s}", align_bytes=64) for s in (0, 2)}
+        words[1] = late.tile([P, T], U32, name="words1", offset=2 * T, align_bytes=64)
+        grouped = {}
         slot_words = {}
         slot_scales = {}
 
-        def quantise(s, half, on_scalar):
-            grouped = keep.tile([P, HALF, 4], BF16, name=f"grouped{s}_{half}", tag=f"grouped{s}_{half}", align_bytes=64)
-            to, frm = interleave_views(grouped[:, 0:on_scalar, :], raw[s, half][:, :, 0:on_scalar])
-            nc.scalar.activation(to, frm, COPY)
+        def round_tokens(s, half, on_scalar):
+            tile = keep.tile([P, HALF, 4], BF16, name=f"grouped{s}_{half}", tag=f"grouped{s}_{half}", align_bytes=64)
+            grouped[s, half] = tile
+            t0 = HALF * half
+            if on_scalar > 0:
+                to, frm = interleave_views(tile[:, 0:on_scalar, :], raw[s][:, :, t0 : t0 + on_scalar])
+                nc.scalar.activation(to, frm, COPY)
             if on_scalar < HALF:
-                to, frm = interleave_views(grouped[:, on_scalar:HALF, :], raw[s, half][:, :, on_scalar:HALF])
+                to, frm = interleave_views(tile[:, on_scalar:HALF, :], raw[s][:, :, t0 + on_scalar : t0 + HALF])
                 nc.vector.tensor_copy(to, frm)
+
+        def round_rows(u, t0, t1, on_scalar):
+            half = t0 // HALF
+            dst_view = grouped[0, half][:, t0 - HALF * half : t1 - HALF * half, 2 * u : 2 * u + 2]
+            to, frm = interleave_views(dst_view, first[u][:, :, t0:t1])
+            if on_scalar:
+                nc.scalar.activation(to, frm, COPY)
+            else:
+                nc.vector.tensor_copy(to, frm)
+
+        def quantise(s, half):
             cols = slice(HALF * half, HALF * (half + 1))
             nc.vector.quantize_mx(
                 out=words[s][:, cols].bitcast(E4M3),
-                scales=scales[s][:, cols],
-                in_=grouped[:].rearrange("p t j -> p (t j)"),
+                scales=planes[s][:, cols],
+                in_=grouped[s, half][:].rearrange("p t j -> p (t j)"),
             )
 
-        def gather_words(s, c0, c1):
-            gathered = keep.tile([P, c1 - c0], U32, name=f"gw{s}_{c0}", tag=f"gw{s}_{c0}", align_bytes=64)
+        def gather_words(s, c0, c1, tag=None):
+            name = f"gw{s}_{c0}"
+            gathered = keep.tile([P, c1 - c0], U32, name=name, tag=tag or name, align_bytes=64)
             nc.vector.tensor_copy(gathered[:], words[s][:].indirect(offs_t[:, c0 // 16 : c1 // 16]))
             for b in range(c0 // P, c1 // P):
                 slot_words[s, b] = gathered[:, P * b - c0 : P * b - c0 + P]
 
-        def gather_scales2(b):
-            gathered = keep.tile([P, P], U8, name=f"gs2_{P * b}", align_bytes=64)
-            nc.vector.tensor_copy(gathered[:], scales2[:].indirect(offs_t[:, P * b // 16 : P * (b + 1) // 16]))
-            slot_scales[2, b] = gathered[:, 0:P]
+        def gather_scales2(c0, c1, tag=None):
+            name = f"gs2_{c0}"
+            gathered = keep.tile([P, c1 - c0], U8, name=name, tag=tag or name, align_bytes=64)
+            nc.vector.tensor_copy(gathered[:], plane2[:].indirect(offs_t[:, c0 // 16 : c1 // 16]))
+            for b in range(c0 // P, c1 // P):
+                slot_scales[2, b] = gathered[:, P * b - c0 : P * b - c0 + P]
 
-        def gather_scales01(e):
-            c0, c1 = C * e, C * (e + 1)
-            gathered = keep.tile([P, C], U8, name=f"gs01_{c0}", align_bytes=64)
-            nc.vector.tensor_copy(gathered[:], scales01[:].indirect(offs_t[:, c0 // 16 : c1 // 16]))
+        def gather_scales01(c0, c1, tag=None):
+            name = f"gs01_{c0}"
+            gathered = keep.tile([P, c1 - c0], U8, name=name, tag=tag or name, align_bytes=64)
+            nc.vector.tensor_copy(gathered[:], plane01[:].indirect(offs_t[:, c0 // 16 : c1 // 16]))
             nc.sync.dma_start(
-                moved0[0:PLANE_ROWS, c0:c1].bitcast(I32), gathered[SHIFT : SHIFT + PLANE_ROWS].bitcast(I32)
+                moved[c0 // C][0:PLANE_ROWS].bitcast(I32), gathered[SHIFT : SHIFT + PLANE_ROWS].bitcast(I32)
             )
             for b in range(c0 // P, c1 // P):
                 slot_scales[1, b] = gathered[:, P * b - c0 : P * b - c0 + P]
-                slot_scales[0, b] = moved0[:, P * b : P * (b + 1)]
+                slot_scales[0, b] = moved[c0 // C][:, P * b - c0 : P * b - c0 + P]
 
         acc = {}
 
@@ -146,50 +162,58 @@ def tile_moe_two_mlp_silu_kernel(
                 out=acc[b][:],
                 lhsT=slot_words[s, b].bitcast(E4M3),
                 lhsT_scale=slot_scales[s, b],
-                rhs=w1_t[e, s].bitcast(E2M1),
+                rhs=w1_t[s][:, e, :].bitcast(E2M1),
                 rhs_scale=w1_sc[:, e * PASSES + s, :],
                 start=(s == PASS_ORDER[0]),
-                stop=(s == PASS_ORDER[-1]),
+                stop=(s == PASSES - 1),
             )
 
-        grouped_h = {}
+        h = {}
+        turned = {}
+        grouped_h = [keep.tile([P, C, 4], BF16, name=f"hgrouped{e}", align_bytes=64) for e in range(E)]
 
-        def hidden(b):
-            h = keep.tile([P, H], BF16, name=f"h{b}", tag=f"h{b}")
+        def silu(b):
+            if b == 3:
+                h[b] = shared.tile([P, H], BF16, name="h3", offset=0, align_bytes=64)
+            else:
+                h[b] = keep.tile([P, H], BF16, name=f"h{b}", align_bytes=64)
             nc.scalar.activation(
-                h[:].rearrange("r (u p d) -> r u p d", u=2, d=2),
+                h[b][:].rearrange("r (u p d) -> r u p d", u=2, d=2),
                 acc[b][:].rearrange("r (p u d) -> r u p d", u=2, d=2),
                 SILU,
             )
-            h_pairs = h[:].bitcast(F32)
-            turned = psum.tile([P, 2, P], F32, name=f"turned{b}", tag=f"turned{b}" if b < 2 else f"bank{b - 2}")
+
+        def turn(b, bank):
+            pairs = h[b][:].bitcast(F32)
+            turned[b] = psum.tile([P, 2, P], F32, name=f"turned{b}", tag=bank)
             for u in range(2):
-                nc.tensor.transpose(turned[:, u, :], h_pairs[:, P * u : P * (u + 1)], ident[:])
-            grouped_h[b] = keep.tile([P, P, 4], BF16, name=f"hgrouped{b}", tag=f"hgrouped{b}", align_bytes=64)
-            pairs = grouped_h[b][:].rearrange("p r f -> p (r f)").bitcast(F32).rearrange("p (r u) -> p r u", u=2)
-            if b == 0:
-                nc.vector.tensor_copy(pairs, turned[:].rearrange("p u r -> p r u"))
+                nc.tensor.transpose(turned[b][:, u, :], pairs[:, P * u : P * (u + 1)], ident[:])
+
+        def copy_turned(b, on_scalar):
+            part = grouped_h[b // 2][:, P * (b % 2) : P * (b % 2 + 1), :]
+            pairs = part.rearrange("p r f -> p (r f)").bitcast(F32).rearrange("p (r u) -> p r u", u=2)
+            if on_scalar:
+                nc.scalar.copy(pairs, turned[b][:].rearrange("p u r -> p r u"))
             else:
-                nc.scalar.copy(pairs, turned[:].rearrange("p u r -> p r u"))
+                nc.vector.tensor_copy(pairs, turned[b][:].rearrange("p u r -> p r u"))
 
         y = {}
+        codes = {}
 
-        def second_layer(b):
-            e = b // 2
-            h_words = keep.tile([P, P], U32, name=f"hw{b}", align_bytes=64)
-            h_scales = keep.tile([P, P], U8, name=f"hsc{b}", tag=f"hsc{b}", align_bytes=64)
+        def second_layer(c0, c1, banks):
+            e = c0 // C
+            h_words = keep.tile([P, c1 - c0], U32, name=f"hw{c0}", align_bytes=64)
+            codes[c0] = h_words
+            h_scales = keep.tile([P, c1 - c0], U8, name=f"hsc{c0}", align_bytes=64)
             nc.vector.quantize_mx(
-                out=h_words[:].bitcast(E4M3), scales=h_scales[:], in_=grouped_h[b][:].rearrange("p r f -> p (r f)")
+                out=h_words[:].bitcast(E4M3),
+                scales=h_scales[:],
+                in_=grouped_h[e][:, c0 - C * e : c1 - C * e, :].rearrange("p r f -> p (r f)"),
             )
-            if b < LAST_TILE:
-                y[b] = psum.tile([P, 2, P], F32, name=f"y{b}", tag=f"y{b}" if b < 2 else "turned0")
-                sums = [y[b][:, nh, :] for nh in range(2)]
-            else:
-                y[b] = [psum.tile([P, P], F32, name=f"y3_{nh}", tag=("turned1", "y0")[nh]) for nh in range(2)]
-                sums = [y[b][nh][:] for nh in range(2)]
             for nh in range(2):
+                y[c0, nh] = psum.tile([P, c1 - c0], F32, name=f"y{c0}_{nh}", tag=banks[nh])
                 nc.tensor.matmul_mx(
-                    out=sums[nh],
+                    out=y[c0, nh][:],
                     lhsT=w2_t[:, e, N * nh : N * (nh + 1)].bitcast(E2M1),
                     lhsT_scale=w2_sc[:, e, P * nh : P * (nh + 1)],
                     rhs=h_words[:].bitcast(E4M3),
@@ -198,78 +222,82 @@ def tile_moe_two_mlp_silu_kernel(
                     stop=True,
                 )
 
-        gated = keep.tile([P, 2, T], F32, name="gated")
-
-        def times_gate(b):
-            nc.vector.tensor_tensor(
-                gated[:, :, P * b : P * (b + 1)],
-                y[b][:],
-                gate_t[:, P * b : P * (b + 1)].unsqueeze(1).broadcast_to([P, 2, P]),
-                MULT,
-            )
-
+        plain = keep.tile([P, T], F32, name="plain")
+        gated = keep.tile([P, T], F32, name="gated")
         placed = {}
 
-        def scatter_on_scalar(nh, c0, c1):
-            nc.scalar.activation(placed[nh][:].indirect(dst_t[:, c0 // 16 : c1 // 16]), gated[:, nh, c0:c1], COPY)
+        def leave_psum(c0, c1):
+            nc.scalar.copy(plain[:, c0:c1], y[c0, 0][:])
+            nc.vector.tensor_tensor(gated[:, c0:c1], y[c0, 1][:], gate_t[:, c0:c1], MULT)
 
-        def scatter_on_vector(nh, c0, c1):
-            nc.vector.tensor_copy(placed[nh][:].indirect(dst_t[:, c0 // 16 : c1 // 16]), gated[:, nh, c0:c1])
+        def scatter_on_scalar(c0, c1):
+            nc.scalar.activation(placed[1][:].indirect(dst_t[:, c0 // 16 : c1 // 16]), gated[:, c0:c1], COPY)
 
-        quantise(0, 0, HALF // 2)
-        quantise(0, 1, HALF // 2)
+        def scatter_on_vector(c0, c1):
+            nc.vector.tensor_tensor(
+                placed[0][:].indirect(dst_t[:, c0 // 16 : c1 // 16]), plain[:, c0:c1], gate_t[:, c0:c1], MULT
+            )
+
+        for half in range(2):
+            grouped[0, half] = keep.tile([P, HALF, 4], BF16, name=f"grouped0_{half}", align_bytes=64)
+        round_rows(0, 0, HALF, False)
+        round_rows(0, HALF, T, True)
+        round_rows(1, 0, HALF, False)
+        round_rows(1, HALF, HALF + 160, True)
+        round_rows(1, HALF + 160, T, False)
+        quantise(0, 0)
+        quantise(0, 1)
         for e in range(E):
             gather_words(0, C * e, C * (e + 1))
-        quantise(1, 0, HALF)
-        quantise(1, 1, HALF // 2)
+        round_tokens(1, 1, 0)
+        round_tokens(1, 0, 224)
+        quantise(1, 1)
+        quantise(1, 0)
         for e in range(E):
-            gather_scales01(e)
+            gather_scales01(C * e, C * (e + 1))
             gather_words(1, C * e, C * (e + 1))
-        w2_t = keep.tile([P, E, 2 * N], U8, name="w2_t", align_bytes=64)
-        for q in range(QUADRANTS):
-            nc.sync.dma_start(
-                w2_sc[32 * q : 32 * q + 4].bitcast(I32),
-                w2_scales[:, 0, 4 * q : 4 * q + 4, :].rearrange("e q n -> q e n").bitcast(I32),
-            )
+        w2_t = late.tile([P, E, 2 * N], U8, name="w2_t", offset=4 * T, align_bytes=64)
         nc.sync.dma_start(w2_t[:], w2_words.rearrange("e s p c -> p (e s) c"))
-        gate_t = keep.tile([P, T], F32, name="gate_t")
+        gate_t = late.tile([P, T], F32, name="gate_t", offset=0, align_bytes=64)
         nc.sync.dma_start(gate_t[:], gate[0:P, :])
-        quantise(2, 0, HALF)
-        quantise(2, 1, HALF)
+        nc.sync.dma_start(dst_t[:], dst)
+        round_tokens(2, 0, HALF)
+        round_tokens(2, 1, HALF)
+        quantise(2, 0)
+        quantise(2, 1)
         for b in range(TILES):
             gather_words(2, P * b, P * (b + 1))
-            gather_scales2(b)
-
+            gather_scales2(P * b, P * (b + 1))
         for b in range(TILES):
-            first_layer(PASS_ORDER[0], b)
-        for s in PASS_ORDER[1:]:
-            for b in (0, 1):
-                first_layer(s, b)
-        hidden(0)
-        hidden(1)
-        for s in PASS_ORDER[1:]:
-            for b in (2, 3):
-                first_layer(s, b)
-        second_layer(0)
-        second_layer(1)
-        hidden(2)
-        hidden(3)
-        times_gate(0)
-        times_gate(1)
-        second_layer(2)
-        second_layer(3)
-        placed[0] = keep.tile([P, T], F32, name="window0", tag="hgrouped2", align_bytes=64)
-        placed[1] = keep.tile([P, T], F32, name="window1")
-        times_gate(2)
-        for nh in range(2):
-            nc.vector.tensor_tensor(
-                gated[:, nh, P * LAST_TILE : T], y[LAST_TILE][nh][:], gate_t[:, P * LAST_TILE : T], MULT
-            )
-
-        scatter_on_vector(1, 0, EARLY_COLUMNS)
-        scatter_on_scalar(0, 0, P)
-        scatter_on_scalar(1, EARLY_COLUMNS, C)
-        scatter_on_scalar(1, C, T)
-        scatter_on_vector(0, P, T)
-        nc.scalar.dma_start(out[P : 2 * P, :], placed[1][:])
+            first_layer(1, b)
+        first_layer(0, 0)
+        first_layer(0, 1)
+        first_layer(2, 0)
+        first_layer(0, 2)
+        first_layer(2, 1)
+        first_layer(0, 3)
+        for b in (0, 1):
+            silu(b)
+            turn(b, f"turned{b}")
+            copy_turned(b, False)
+        for b in (2, 3):
+            first_layer(2, b)
+        second_layer(0, P, ("y0", "y1"))
+        for b in (2, 3):
+            silu(b)
+            turn(b, f"bank{b - 2}")
+            if b == 3:
+                leave_psum(0, P)
+            copy_turned(b, True)
+        second_layer(P, C, ("bank2", "bank3"))
+        second_layer(C, T, ("turned0", "turned1"))
+        placed[0] = keep.tile([P, T], F32, name="window0")
+        placed[1] = shared.tile([P, T], F32, name="window1", offset=0, align_bytes=64)
+        scatter_on_vector(0, P)
+        scatter_on_scalar(0, P)
+        for c0, c1 in ((P, C), (C, T)):
+            leave_psum(c0, c1)
+            scatter_on_vector(c0, c1)
+            scatter_on_scalar(c0, c1)
         nc.sync.dma_start(out[0:P, :], placed[0][:])
+        nc.scalar.dma_start(out[P : 2 * P, :], placed[1][:])

from contextlib import ExitStack

import concourse.mybir as mybir
from concourse.masks import make_identity

K, T, E, C, H, N = 1536, 512, 2, 256, 512, 256
FLOPS = 2 * E * C * (K * H + H * N)

F32 = mybir.dt.float32
BF16 = mybir.dt.bfloat16
I32 = mybir.dt.int32
U32 = mybir.dt.uint32
U16 = mybir.dt.uint16
U8 = mybir.dt.uint8
E4M3 = mybir.dt.float8_e4m3fn_x4
E2M1 = mybir.dt.float4_e2m1fn_x4
COPY = mybir.ActivationFunctionType.Copy
SILU = mybir.ActivationFunctionType.Silu
MULT = mybir.AluOpType.mult

P = 128
PASSES = K // 512
TILES = E * C // P
HALF = T // 2
ROWS = 4
SHIFT = 4
PLANE_ROWS = 100
PASS_ORDER = (1, 0, 2)


def interleave_views(dst, src):
    return (
        dst.rearrange("p (c i) j -> p c j i", i=4),
        src.rearrange("p j (c i) -> p c j i", i=4),
    )


def tile_moe_two_mlp_silu_kernel(
    tc, xT, w1_words, w1_scales, w2_words, w2_scales, gate, offs, dst, out
):
    nc = tc.nc
    with ExitStack() as ctx:
        keep = ctx.enter_context(tc.tile_pool(name="keep", bufs=1))
        shared = ctx.enter_context(tc.tile_pool(name="shared", bufs=1))
        late = ctx.enter_context(tc.tile_pool(name="late", bufs=1))
        psum = ctx.enter_context(tc.psum_pool(name="psum", bufs=1))

        offs_t = keep.tile([P, T // 16], U16, name="offs_t")
        dst_t = keep.tile([P, T // 16], U16, name="dst_t")
        w1_sc = keep.tile([P, E * PASSES, H], U8, name="w1_sc", align_bytes=64)
        nc.vector.memset(w1_sc[:].rearrange("p e i -> p (e i)").bitcast(I32), 0)
        w2_sc = keep.tile([P, E, N], U8, name="w2_sc", align_bytes=64)
        nc.gpsimd.memset(w2_sc[:].rearrange("p e i -> p (e i)").bitcast(I32), 0)
        plane01 = keep.tile([P, T], U8, name="plane01", tag="plane01", align_bytes=64)
        plane2 = keep.tile([P, T], U8, name="plane2", align_bytes=64)
        moved = [keep.tile([P, C], U8, name=f"moved{e}", align_bytes=64) for e in range(E)]
        for plane in (plane01, plane2, *moved):
            nc.gpsimd.memset(plane[:].bitcast(I32), 0)
        planes = [plane01[SHIFT:P], plane01[:], plane2[:]]

        raw = {}

        def load_x(s):
            raw[s] = keep.tile([P, 4, T], F32, name=f"raw{s}", align_bytes=64)
            nc.sync.dma_start(raw[s][:], xT[512 * s : 512 * (s + 1), :].rearrange("(p j) t -> p j t", j=4))

        first = []
        for u in range(2):
            first.append(keep.tile([P, 2, T], F32, name=f"first{u}", align_bytes=64))
            nc.sync.dma_start(first[u][:], xT[0:512, :].rearrange("(p j) t -> p j t", j=4)[:, 2 * u : 2 * u + 2, :])
        nc.sync.dma_start(offs_t[:], offs)
        for r in range(ROWS):
            nc.sync.dma_start(
                w2_sc[r:P:32].bitcast(I32),
                w2_scales[:, 0, r:16:4, :].rearrange("e q n -> q e n").bitcast(I32),
            )
        load_x(1)
        load_x(2)
        for r in range(ROWS):
            nc.sync.dma_start(
                w1_sc[r:P:32].bitcast(I32),
                w1_scales[:, :, r:16:4, :].rearrange("e s q i -> q (e s) i").bitcast(I32),
            )
        w1_t = {}
        for s in PASS_ORDER:
            w1_t[s] = keep.tile([P, E, 2 * H], U8, name=f"w1_{s}", align_bytes=64)
            nc.sync.dma_start(w1_t[s][:], w1_words[:, s].rearrange("e p c -> p e c"))

        ident = keep.tile([P, P], F32, name="ident")
        make_identity(nc, ident[:])
        warm = keep.tile([P, 1], F32, name="warm")
        nc.gpsimd.memset(warm[:], 0.0)
        warm_out = keep.tile([P, 1], F32, name="warm_out")
        nc.scalar.activation(warm_out[:], warm[:], SILU)

        words = {s: keep.tile([P, T], U32, name=f"words{s}", align_bytes=64) for s in (0, 2)}
        words[1] = late.tile([P, T], U32, name="words1", offset=2 * T, align_bytes=64)
        grouped = {}
        slot_words = {}
        slot_scales = {}

        def round_tokens(s, half, on_scalar):
            tile = keep.tile([P, HALF, 4], BF16, name=f"grouped{s}_{half}", tag=f"grouped{s}_{half}", align_bytes=64)
            grouped[s, half] = tile
            t0 = HALF * half
            if on_scalar > 0:
                to, frm = interleave_views(tile[:, 0:on_scalar, :], raw[s][:, :, t0 : t0 + on_scalar])
                nc.scalar.activation(to, frm, COPY)
            if on_scalar < HALF:
                to, frm = interleave_views(tile[:, on_scalar:HALF, :], raw[s][:, :, t0 + on_scalar : t0 + HALF])
                nc.vector.tensor_copy(to, frm)

        def round_rows(u, t0, t1, on_scalar):
            half = t0 // HALF
            dst_view = grouped[0, half][:, t0 - HALF * half : t1 - HALF * half, 2 * u : 2 * u + 2]
            to, frm = interleave_views(dst_view, first[u][:, :, t0:t1])
            if on_scalar:
                nc.scalar.activation(to, frm, COPY)
            else:
                nc.vector.tensor_copy(to, frm)

        def quantise(s, half):
            cols = slice(HALF * half, HALF * (half + 1))
            nc.vector.quantize_mx(
                out=words[s][:, cols].bitcast(E4M3),
                scales=planes[s][:, cols],
                in_=grouped[s, half][:].rearrange("p t j -> p (t j)"),
            )

        def gather_words(s, c0, c1, tag=None):
            name = f"gw{s}_{c0}"
            gathered = keep.tile([P, c1 - c0], U32, name=name, tag=tag or name, align_bytes=64)
            nc.vector.tensor_copy(gathered[:], words[s][:].indirect(offs_t[:, c0 // 16 : c1 // 16]))
            for b in range(c0 // P, c1 // P):
                slot_words[s, b] = gathered[:, P * b - c0 : P * b - c0 + P]

        def gather_scales2(c0, c1, tag=None):
            name = f"gs2_{c0}"
            gathered = keep.tile([P, c1 - c0], U8, name=name, tag=tag or name, align_bytes=64)
            nc.vector.tensor_copy(gathered[:], plane2[:].indirect(offs_t[:, c0 // 16 : c1 // 16]))
            for b in range(c0 // P, c1 // P):
                slot_scales[2, b] = gathered[:, P * b - c0 : P * b - c0 + P]

        def gather_scales01(c0, c1, tag=None):
            name = f"gs01_{c0}"
            gathered = keep.tile([P, c1 - c0], U8, name=name, tag=tag or name, align_bytes=64)
            nc.vector.tensor_copy(gathered[:], plane01[:].indirect(offs_t[:, c0 // 16 : c1 // 16]))
            nc.sync.dma_start(
                moved[c0 // C][0:PLANE_ROWS].bitcast(I32), gathered[SHIFT : SHIFT + PLANE_ROWS].bitcast(I32)
            )
            for b in range(c0 // P, c1 // P):
                slot_scales[1, b] = gathered[:, P * b - c0 : P * b - c0 + P]
                slot_scales[0, b] = moved[c0 // C][:, P * b - c0 : P * b - c0 + P]

        acc = {}

        def first_layer(s, b):
            e = b // 2
            if s == PASS_ORDER[0]:
                acc[b] = psum.tile([P, H], F32, name=f"acc{b}", tag=f"bank{b}")
            nc.tensor.matmul_mx(
                out=acc[b][:],
                lhsT=slot_words[s, b].bitcast(E4M3),
                lhsT_scale=slot_scales[s, b],
                rhs=w1_t[s][:, e, :].bitcast(E2M1),
                rhs_scale=w1_sc[:, e * PASSES + s, :],
                start=(s == PASS_ORDER[0]),
                stop=(s == PASSES - 1),
            )

        h = {}
        turned = {}
        grouped_h = [keep.tile([P, C, 4], BF16, name=f"hgrouped{e}", align_bytes=64) for e in range(E)]

        def silu(b):
            if b == 3:
                h[b] = shared.tile([P, H], BF16, name="h3", offset=0, align_bytes=64)
            else:
                h[b] = keep.tile([P, H], BF16, name=f"h{b}", align_bytes=64)
            nc.scalar.activation(
                h[b][:].rearrange("r (u p d) -> r u p d", u=2, d=2),
                acc[b][:].rearrange("r (p u d) -> r u p d", u=2, d=2),
                SILU,
            )

        def turn(b, bank):
            pairs = h[b][:].bitcast(F32)
            turned[b] = psum.tile([P, 2, P], F32, name=f"turned{b}", tag=bank)
            for u in range(2):
                nc.tensor.transpose(turned[b][:, u, :], pairs[:, P * u : P * (u + 1)], ident[:])

        def copy_turned(b, on_scalar):
            part = grouped_h[b // 2][:, P * (b % 2) : P * (b % 2 + 1), :]
            pairs = part.rearrange("p r f -> p (r f)").bitcast(F32).rearrange("p (r u) -> p r u", u=2)
            if on_scalar:
                nc.scalar.copy(pairs, turned[b][:].rearrange("p u r -> p r u"))
            else:
                nc.vector.tensor_copy(pairs, turned[b][:].rearrange("p u r -> p r u"))

        y = {}
        codes = {}

        def second_layer(c0, c1, banks):
            e = c0 // C
            h_words = keep.tile([P, c1 - c0], U32, name=f"hw{c0}", align_bytes=64)
            codes[c0] = h_words
            h_scales = keep.tile([P, c1 - c0], U8, name=f"hsc{c0}", align_bytes=64)
            nc.vector.quantize_mx(
                out=h_words[:].bitcast(E4M3),
                scales=h_scales[:],
                in_=grouped_h[e][:, c0 - C * e : c1 - C * e, :].rearrange("p r f -> p (r f)"),
            )
            for nh in range(2):
                y[c0, nh] = psum.tile([P, c1 - c0], F32, name=f"y{c0}_{nh}", tag=banks[nh])
                nc.tensor.matmul_mx(
                    out=y[c0, nh][:],
                    lhsT=w2_t[:, e, N * nh : N * (nh + 1)].bitcast(E2M1),
                    lhsT_scale=w2_sc[:, e, P * nh : P * (nh + 1)],
                    rhs=h_words[:].bitcast(E4M3),
                    rhs_scale=h_scales[:],
                    start=True,
                    stop=True,
                )

        plain = keep.tile([P, T], F32, name="plain")
        gated = keep.tile([P, T], F32, name="gated")
        placed = {}

        def leave_psum(c0, c1):
            nc.scalar.copy(plain[:, c0:c1], y[c0, 0][:])
            nc.vector.tensor_tensor(gated[:, c0:c1], y[c0, 1][:], gate_t[:, c0:c1], MULT)

        def scatter_on_scalar(c0, c1):
            nc.scalar.activation(placed[1][:].indirect(dst_t[:, c0 // 16 : c1 // 16]), gated[:, c0:c1], COPY)

        def scatter_on_vector(c0, c1):
            nc.vector.tensor_tensor(
                placed[0][:].indirect(dst_t[:, c0 // 16 : c1 // 16]), plain[:, c0:c1], gate_t[:, c0:c1], MULT
            )

        for half in range(2):
            grouped[0, half] = keep.tile([P, HALF, 4], BF16, name=f"grouped0_{half}", align_bytes=64)
        round_rows(0, 0, HALF, False)
        round_rows(0, HALF, T, True)
        round_rows(1, 0, HALF, False)
        round_rows(1, HALF, HALF + 160, True)
        round_rows(1, HALF + 160, T, False)
        quantise(0, 0)
        quantise(0, 1)
        for e in range(E):
            gather_words(0, C * e, C * (e + 1))
        round_tokens(1, 1, 0)
        round_tokens(1, 0, 224)
        quantise(1, 1)
        quantise(1, 0)
        for e in range(E):
            gather_scales01(C * e, C * (e + 1))
            gather_words(1, C * e, C * (e + 1))
        w2_t = late.tile([P, E, 2 * N], U8, name="w2_t", offset=4 * T, align_bytes=64)
        nc.sync.dma_start(w2_t[:], w2_words.rearrange("e s p c -> p (e s) c"))
        gate_t = late.tile([P, T], F32, name="gate_t", offset=0, align_bytes=64)
        nc.sync.dma_start(gate_t[:], gate[0:P, :])
        nc.sync.dma_start(dst_t[:], dst)
        round_tokens(2, 0, HALF)
        round_tokens(2, 1, HALF)
        quantise(2, 0)
        quantise(2, 1)
        for b in range(TILES):
            gather_words(2, P * b, P * (b + 1))
            gather_scales2(P * b, P * (b + 1))
        for b in range(TILES):
            first_layer(1, b)
        first_layer(0, 0)
        first_layer(0, 1)
        first_layer(2, 0)
        first_layer(0, 2)
        first_layer(2, 1)
        first_layer(0, 3)
        for b in (0, 1):
            silu(b)
            turn(b, f"turned{b}")
            copy_turned(b, False)
        for b in (2, 3):
            first_layer(2, b)
        second_layer(0, P, ("y0", "y1"))
        for b in (2, 3):
            silu(b)
            turn(b, f"bank{b - 2}")
            if b == 3:
                leave_psum(0, P)
            copy_turned(b, True)
        second_layer(P, C, ("bank2", "bank3"))
        second_layer(C, T, ("turned0", "turned1"))
        placed[0] = keep.tile([P, T], F32, name="window0")
        placed[1] = shared.tile([P, T], F32, name="window1", offset=0, align_bytes=64)
        scatter_on_vector(0, P)
        scatter_on_scalar(0, P)
        for c0, c1 in ((P, C), (C, T)):
            leave_psum(c0, c1)
            scatter_on_vector(c0, c1)
            scatter_on_scalar(c0, c1)
        nc.sync.dma_start(out[0:P, :], placed[0][:])
        nc.scalar.dma_start(out[P : 2 * P, :], placed[1][:])
